import numpy as np, ml_dtypes
CORES = [16,18,20,22]
N = 4
BF = ml_dtypes.bfloat16
S, SL, W, LN, CAP, T = 4, 1024, 4096, 2, 320, 5
def parts(rng):
    x = rng.integers(0, 256, (N, 8, 16, W)); ga = rng.integers(0, 4, (N, 8, 16, 16)); ha = rng.integers(0, 4, (N, 8, 16, 16))
    w = rng.integers(0, 256, (N, 8, 16)) << rng.integers(0, 5, (N, 8, 16)); od = rng.integers(0, 16, (N, 8))
    np.put_along_axis(w, od[:, :, None], 2 * rng.integers(0, 128, (N, 8, 1)) + 1, 2)
    return x, ga, ha, w, od
def pack(x, ga, ha, w):
    def full(b):
        z = np.zeros((N, 8, 16, 8, 16), np.float32)
        for g in range(8): z[:, g, :, g, :] = b[:, g]
        return z.reshape(N, 128, 128).astype(BF)
    return {"m": np.ascontiguousarray(x.reshape(N, 128, W)).astype(np.float32).astype(BF), "gm": full(ga), "hm": full(ha), "kw": w.reshape(N, 128, 1).astype(np.float32).astype(BF)}
def steer(x, w, i, q, g, cols, who):
    b = x[q, g][:, cols].copy(); b[i] -= b[i] & (N - 1)
    b[i] += (w[q, g, i] * (who - np.dot(w[q, g], b))) & (N - 1)
    x[q, g][:, cols] = b
def nail(x, w, i, k, q, g, cols, goal):
    b = x[q, g][:, cols].copy(); b[i] = 0; b[k] = 0
    v = (goal - np.dot(w[q, g], b)) & 65535; b[i] = v & 255; b[k] = v >> 8
    x[q, g][:, cols] = b
def still(o, q, g, ga, ha, w):
    w[q, g, o[8:]] = 0; ga[q, g][:, o[:8]] = 0; ha[q, g][:, o[:8]] = 0
def setup_inputs(rng):
    x, ga, ha, w, od = parts(rng)
    for q in range(N):
        for g in range(8):
            n = int(rng.integers(0, SL + 1)); steer(x, w, od[q, g], q, g, W - SL + rng.permutation(SL)[:n], int(rng.integers(0, N)))
        g = int(rng.integers(0, 8)); w[q, g] -= w[q, g] & 1
    return pack(x, ga, ha, w)
def setup_inputs_room(rng):
    x, ga, ha, w, od = parts(rng)
    for q in range(N):
        for g in range(8):
            if g % 2 == 0:
                o = rng.permutation(16); od[q, g] = o[0]; w[q, g, o[0]] = 2 * rng.integers(0, 128) + 1; still(o, q, g, ga, ha, w)
            for s in range(S):
                other = (q + 1 + rng.permutation(N - 1)) % N
                if q == 0: other = np.concatenate([np.array([1]), other[other != 1]])
                who = np.full(SL, q); at = 0
                for d in range(N - 1):
                    n = int(rng.choice(np.array([0, 1, CAP - 1, CAP, CAP + 1, CAP, CAP + 1, SL])))
                    if q == 0 and d == 0: n = (CAP, CAP + 1, SL, CAP - 1, CAP + 1, 0, 1, CAP)[g]
                    n = min(n, SL - at); who[at:at + n] = other[d]; at += n
                steer(x, w, od[q, g], q, g, s * SL + rng.permutation(SL), who)
    return pack(x, ga, ha, w)
def setup_inputs_full(rng):
    x, ga, ha, w, od = parts(rng); z = int(rng.integers(0, N)); p = rng.permutation(N)
    for q in range(N):
        for g in range(8):
            o = rng.permutation(16); od[q, g] = o[0]; w[q, g, o[0]] = 2 * rng.integers(0, 128) + 1; still(o, q, g, ga, ha, w)
            for s in range(S):
                if s == S - 1:
                    other = (q + 1 + rng.permutation(N - 1)) % N
                    if q != z: other = np.concatenate([np.array([z]), other[other != z]])
                    who = rng.permutation(np.repeat(other, CAP)[:SL]); who = np.concatenate([who, np.full(SL - len(who), q)])
                elif (p[q] + s) % 2 == 0: who = np.full(SL, q)
                else: who = np.full(SL, (q + int(rng.integers(1, N))) % N)
                steer(x, w, od[q, g], q, g, s * SL + np.arange(SL), who)
    return pack(x, ga, ha, w)
def setup_inputs_alike(rng):
    x, ga, ha, w, od = parts(rng); j = np.arange(SL)
    for q in range(N):
        for g in range(8):
            o = rng.permutation(16); w[q, g, o[0]] = 1; w[q, g, o[1]] = 256
            if g % 2 == 1: still(o, q, g, ga, ha, w)
            for s in range(S):
                cols = s * SL + j; nx = (s + 1) % S
                if g < 2: goal = rng.choice(np.array([0, N * W - 1, q, (W - 1) * N + q, int(rng.integers(0, N * W)), int(rng.integers(0, N * W))]), SL)
                elif g < 4: goal = (nx * SL + np.where(rng.random(SL) < 0.5, j, SL - 1 - j)) * N + np.where(rng.random(SL) < 0.3, q, rng.integers(0, N, SL))
                elif g < 6: goal = (s * SL + j) * N + rng.integers(0, N, SL)
                else: goal = np.full(SL, int(rng.integers(0, W)) * N + (q + 1) % N)
                if g == 6: x[q, g][:, cols] = x[q, g][:, s * SL:s * SL + 1]
                nail(x, w, o[0], o[1], q, g, cols, goal)
    return pack(x, ga, ha, w)
def setup_inputs_ends(rng):
    x, ga, ha, w, od = parts(rng)
    for q in range(N):
        z = rng.permutation(8)
        w[q, z[0]] = 0
        w[q, z[1]] = 4080; x[q, z[1]] = 255; ga[q, z[1]] = 3; ha[q, z[1]] = 3
        x[q, z[2]] = 0
        ga[q, z[3]] = 0; ha[q, z[3]] = 0
        ga[q, z[4]] = 0; ha[q, z[4]] = np.eye(16, dtype=np.int64)
        x[q, z[5]] = 255 * rng.integers(0, 2, (16, W)); ga[q, z[5]] = 3 * rng.integers(0, 2, (16, 16)); ha[q, z[5]] = 3 * rng.integers(0, 2, (16, 16))
        w[q, z[6]] = 0; w[q, z[6], od[q, z[6]]] = 1; ga[q, z[6]] = 3; ha[q, z[6]] = 3
        o = rng.permutation(16); big = o[:14]; g = int(z[7])
        w[q, g, big] = 16 * rng.integers(188, 256, 14); w[q, g, o[14:]] = 2 * rng.integers(0, 128, 2) + 1
        x[q, g] = rng.integers(200, 256, (16, W)); ga[q, g][:, big] = 0; ha[q, g][:, big] = 0
    return pack(x, ga, ha, w)
def setup_inputs_spread(rng):
    x, ga, ha, w, od = parts(rng)
    x = np.minimum((np.exp2(8 * rng.random((N, 8, 1, W))) * rng.random((N, 8, 16, W))).astype(np.int64), 255)
    w = (rng.integers(0, 256, w.shape) >> rng.integers(0, 8, w.shape)) << rng.integers(0, 5, w.shape)
    np.put_along_axis(w, od[:, :, None], 2 * rng.integers(0, 128, (N, 8, 1)) + 1, 2)
    ga = np.where(rng.random(ga.shape) < 0.1 + 0.9 * rng.random((N, 8, 1, 1)), ga, 0); ha = np.where(rng.random(ha.shape) < 0.1 + 0.9 * rng.random((N, 8, 1, 1)), ha, 0)
    return pack(x, ga, ha, w)
def check_inputs(d):
    bad = []
    for k, hi in (("m", 255), ("gm", 3), ("hm", 3), ("kw", 4080)):
        v = np.asarray(d[k]).astype(np.float64)
        if not np.all((v >= 0) & (v <= hi) & (v == np.floor(v))): bad.append("range of " + k)
    p = np.arange(128) >> 4; off = p[:, None] != p[None, :]
    for k in ("gm", "hm"):
        if np.any(np.asarray(d[k]).astype(np.float64)[:, off] != 0): bad.append("blocks of " + k)
    return bad
def reference(m, gm, hm, kw):
    x = m.astype(np.float32).astype(np.int64).reshape(N, 8, 16, W); w = kw.astype(np.float32).astype(np.int64).reshape(N, 8, 16, 1)
    gt = np.swapaxes(gm.astype(np.float64), 1, 2); ht = np.swapaxes(hm.astype(np.float64), 1, 2)
    me = np.eye(N, dtype=bool)[:, None, :, None]; gi = np.arange(8)[None, :, None]
    for t in range(T):
        s = t % S; lo = s * SL; pl = ((s + S - 1) % S) * SL
        prev = x[..., pl:pl + SL]; a = np.add.reduce(prev * w, axis=2)
        who = a & (N - 1); blk = (a >> LN) & (W - 1)
        h = who[:, :, None, :] == np.arange(N)[None, None, :, None]
        cnt = np.add.accumulate(h.astype(np.int64), axis=3)
        ok = np.any(h & ((cnt <= CAP) | me), axis=2)
        ref = np.swapaxes(x[who, gi, :, blk], 2, 3) * ok[:, :, None, :]
        new = np.matmul(gt, prev.reshape(N, 128, SL).astype(np.float64)) + np.matmul(ht, ref.reshape(N, 128, SL).astype(np.float64))
        x[..., lo:lo + SL] = (new.astype(np.int64).reshape(N, 8, 16, SL) + x[..., lo:lo + SL]) & 255
    return {"y": x.reshape(N, 128, W).astype(np.float32).astype(BF)}

@@ -1,0 +1,373 @@
+from concourse.bass import DstId, RemoteDMATransfer
+from concourse.mybir import AluOpType as A, ActivationFunctionType as F
+
+S, SL, HB, WAVES, CAP = 4, 1024, 512, 5, 320
+Z = 16
+VB = 4096
+KH = 1024.0
+LIFT = 129.0 * 256.0
+
+SCRATCH = {
+    "win": ("sbuf", [128, Z + 9 * VB], "bfloat16"),
+    "oth": ("sbuf", [128, S * HB], "bfloat16"),
+    "back": ("sbuf", [128, S * HB], "bfloat16"),
+    "pk": ("sbuf", [128, 272], "bfloat16"),
+    "pkp": ("sbuf", [128, 272], "bfloat16"),
+    "gh": ("sbuf", [128, 512], "bfloat16"),
+    "wc": ("sbuf", [128, 16], "float32"),
+    "wb": ("sbuf", [128, 288], "bfloat16"),
+    "ref": ("sbuf", [128, SL], "bfloat16"),
+    "rnd": ("sbuf", [128, SL], "bfloat16"),
+    "lift": ("sbuf", [128, 256], "bfloat16"),
+    "mats": ("sbuf", [128, 8 * 128], "bfloat16"),
+    "ci": ("sbuf", [128, 8], "int32"),
+    "cf": ("sbuf", [128, 8], "float32"),
+    "mi": ("sbuf", [128, 192], "int32"),
+    "mj": ("sbuf", [128, 320], "int32"),
+    "mf": ("sbuf", [128, 144], "float32"),
+    "rst": ("sbuf", [128, 192], "bfloat16"),
+    "xi": ("sbuf", [128, 7 * 64], "int32"),
+    "xf": ("sbuf", [128, 5 * 64], "float32"),
+    "hh": ("sbuf", [128, 192], "bfloat16"),
+    "sf": ("sbuf", [128, 192], "bfloat16"),
+    "sb": ("sbuf", [128, 192], "bfloat16"),
+    "uu": ("sbuf", [128, 192], "float32"),
+    "off": ("sbuf", [128, 64], "uint16"),
+}
+for _n in ("px0", "px1", "px2", "px3", "pa", "pc", "ps0", "ps1"):
+    SCRATCH[_n] = ("psum", [128, 512], "float32")
+SEMAPHORES = (["sv", "sa", "sp", "sg", "sent", "stored", "lpk", "apk"]
+              + ["lw%d" % s for s in range(S)] + ["lo%d" % s for s in range(S)]
+              + ["in%d_%d" % (s, r) for s in range(S) for r in range(4)]
+              + ["wv%d_%d" % (t, b) for t in range(WAVES - 1) for b in range(2)]
+              + ["bk%d" % t for t in range(1, WAVES)])
+
+
+def col(v, swapped, who):
+    return Z + v * VB + swapped * 2048 + who * HB
+
+
+def rank_program(g, core, T, topo):
+    r = T.rank_of(core)
+    if r is None:
+        return
+    cores = list(T.cores)
+    sets = [[q for q in range(4) if topo.die(cores[q]) == topo.die(cores[0])],
+            [q for q in range(4) if topo.die(cores[q]) != topo.die(cores[0])]]
+    M = 0 if r in sets[0] else 1
+    pos = sets[M].index(r)
+    mate, part, pmate = sets[M][1 - pos], sets[1 - M][pos], sets[1 - M][1 - pos]
+    mine = [part, r]
+    theirs = [pmate, mate]
+
+    def dst(q):
+        rid, pid, _ = topo.addr(cores[q])
+        return DstId(rid=rid, pnc=pid)
+
+    def bits(es):
+        return sum(1 << e for e in es)
+
+    V, AC, PE, SY = g.vector, g.scalar, g.tensor, g.sync
+    Q = {"v": [V, "sv", 0, {}], "a": [AC, "sa", 0, {}], "p": [PE, "sp", 0, {}], "g": [g, "sg", 0, {}],
+         "s": [SY, None, 0, {}]}
+
+    def wait(qn, deps):
+        q = Q[qn]
+        for d in deps:
+            if d is not None and q[3].get(d[0], 0) < d[1]:
+                q[0].wait_ge(T.sem[d[0]], d[1])
+                q[3][d[0]] = d[1]
+
+    def done(qn, inst):
+        q = Q[qn]
+        inst.then_inc(T.sem[q[1]], 1)
+        q[2] += 1
+        return (q[1], q[2])
+
+    def ts(out, in0, s1, op0, s2=None, op1=None, deps=()):
+        wait("v", deps)
+        if op1 is None:
+            return done("v", V.tensor_scalar(out, in0, s1, None, op0))
+        return done("v", V.tensor_scalar(out, in0, s1, s2, op0, op1))
+
+    def tt(out, a, b, op, deps=()):
+        wait("v", deps)
+        return done("v", V.tensor_tensor(out, a, b, op))
+
+    def cp(out, a, deps=()):
+        wait("v", deps)
+        return done("v", V.tensor_copy(out, a))
+
+    def acp(out, a, deps=()):
+        wait("a", deps)
+        return done("a", AC.activation(out, a, F.Copy))
+
+    def fill(ap, c, deps=()):
+        wait("v", deps)
+        return done("v", V.memset(ap, c))
+
+    def mm(items, deps=()):
+        wait("p", deps)
+        inst = None
+        for out, lhsT, rhs, st, sp in items:
+            inst = PE.matmul(out, lhsT, rhs, st, sp)
+        return done("p", inst)
+
+    W = T.win
+    sent = [0]
+
+    def send(transfers, n, deps):
+        wait("g", deps)
+        g.remote_dma_fused(transfers, local_sem=T.sem.sent)
+        sent[0] += n
+
+    def half(p):
+        return slice(64 * p, 64 * p + 64)
+
+    order = [3, 0, 1, 2]
+    t_pad = fill(T.pk[:, 256:272], 0.0)
+    AC.dma_start(T.pk[:, 0:128], T.gm[:]).then_inc(T.sem.lpk, 16)
+    AC.dma_start(T.pk[:, 128:256], T.hm[:]).then_inc(T.sem.lpk, 16)
+    wait("a", [t_pad])
+    AC.dma_start(T.pk[:, 256:257], T.kw[:]).then_inc(T.sem.lpk, 16)
+    for n, s in enumerate(order):
+        dq = AC if n % 2 else SY
+        c = col(s, 0, r)
+        for p in range(2):
+            src = slice(s * SL + p * HB, s * SL + (p + 1) * HB)
+            dq.dma_start(T.oth[half(p), s * HB:(s + 1) * HB], T.m[half(1 - M), src]).then_inc(T.sem["lo%d" % s], 16)
+        for p in range(2):
+            src = slice(s * SL + p * HB, s * SL + (p + 1) * HB)
+            dq.dma_start(W[half(p), c:c + HB], T.m[half(M), src]).then_inc(T.sem["lw%d" % s], 16)
+
+    t_ci = done("g", g.iota(T.ci[:, 0:2], [[64, 2]], 0, 1))
+    t_mi = done("g", g.iota(T.mi[:], [[1, 192]], 0, 0))
+    t_z = fill(W[:, 0:Z], 0.0)
+    t_gh0 = fill(T.gh[:], 0.0)
+    fill(T.lift[:], LIFT)
+    ts(T.ci[:, 2:3], T.ci[:, 1:2], 127, A.bitwise_and, deps=[t_ci])
+    ts(T.ci[:, 3:4], T.ci[:, 0:1], 4, A.logical_shift_right, 3, A.bitwise_and)
+    ts(T.ci[:, 4:5], T.ci[:, 0:1], 112, A.bitwise_and)
+    k = ts(T.ci[:, 5:6], T.ci[:, 0:1], 6, A.logical_shift_right)
+    k_mf = cp(T.mf[:], T.mi[:, 0:144], deps=[t_mi])
+    ts(T.mj[:, 0:128], T.mi[:, 0:128], 4, A.logical_shift_right, 3, A.bitwise_and)
+    k_mj = ts(T.mj[:, 128:320], T.mi[:], 31, A.bitwise_and)
+    k = cp(T.cf[:, 0:6], T.ci[:, 0:6], deps=[k])
+    pf, px, pg, ph = T.cf[:, 0:1], T.cf[:, 2:3], T.cf[:, 3:4], T.cf[:, 5:6]
+    ID, PM, M1, M2, M3, NS, LT, KI = [T.mats[:, i * 128:(i + 1) * 128] for i in range(8)]
+    t_pm = ts(PM, T.mf[:, 0:128], px, A.is_equal, deps=[k, k_mf])
+    ts(T.cf[:, 6:7], T.cf[:, 4:5], 15.0, A.add)
+    k_cf = ts(T.cf[:, 7:8], ph, 2048.0, A.mult)
+    p15, flip = T.cf[:, 6:7], T.cf[:, 7:8]
+
+    def stationaries(R, pk, deps):
+        for p in range(2):
+            for i in range(2):
+                cp(T.gh[half(p), (2 * R + i) * 128 + 64 * p:(2 * R + i) * 128 + 64 * p + 64],
+                   pk[half(M), i * 128 + 64 * M:i * 128 + 64 * M + 64], deps=deps)
+            k2 = cp(T.wc[half(p), 8 * R:8 * R + 1], pk[half(M), 256:257])
+        return ts(T.wb[:, R * 144:(R + 1) * 144], T.mf[:], p15, A.is_equal, T.wc[:, 8 * R:8 * R + 1], A.mult,
+                  deps=[k2, k_cf])
+
+    ts(ID, T.mf[:, 0:128], pf, A.is_equal)
+    ts(M1, T.mj[:, 0:128], pg, A.is_equal, deps=[k_mj])
+    ts(NS, T.mj[:, 0:128], pg, A.is_equal, -1.0, A.mult)
+    ts(LT, T.mf[:, 0:128], pf, A.is_lt)
+    ts(KI, T.mf[:, 0:128], pf, A.is_equal, KH, A.mult)
+    fill(M2, 0.0)
+    k = ts(T.rst[:], T.mj[:, 128:320], 0.0, A.is_gt)
+    k = tt(LT, LT, NS, A.mult, deps=[k])
+    cp(T.mats[0:64, 3 * 128 + 64:4 * 128], T.mats[0:64, 2 * 128 + 64:3 * 128])
+    fill(T.mats[64:128, 2 * 128:2 * 128 + 64], 0.0)
+    k = tt(M3, LT, KI, A.add, deps=[k])
+    fill(T.mats[64:128, 4 * 128:4 * 128 + 64], 0.0, deps=[k])
+    cp(T.mats[0:64, 4 * 128 + 64:5 * 128], T.mats[0:64, 5 * 128 + 64:6 * 128])
+    t_w1 = stationaries(1, T.pk, [("lpk", 48), t_gh0])
+
+    every = topo.engines(core, cores[part])
+    send([RemoteDMATransfer(dst_ids=[dst(part)], dma_engine_mask=bits(every), remote_sem=T.sem.apk,
+                            src=T.pk[:], dst=T.pkp[:])], len(every), [("lpk", 48)])
+    for n, s in enumerate(order):
+        far = topo.engines(core, cores[part])[n % 2::2]
+        near = topo.engines(core, cores[mate])[1 - n % 2::2]
+        c = col(s, 0, r)
+        sem = T.sem["in%d_%d" % (s, r)]
+        send([RemoteDMATransfer(dst_ids=[dst(part), dst(pmate)], dma_engine_mask=bits(far), remote_sem=sem,
+                                src=T.oth[:, s * HB:(s + 1) * HB], dsts=[W[:, c:c + HB], W[:, c:c + HB]]),
+              RemoteDMATransfer(dst_ids=[dst(mate)], dma_engine_mask=bits(near), remote_sem=sem,
+                                src=W[:, c:c + HB], dst=W[:, c:c + HB])],
+             len(far) + len(near), [("lo%d" % s, 32), ("lw%d" % s, 32)])
+
+    def arrived(s, q):
+        if q == r:
+            return ("lw%d" % s, 32)
+        return ("in%d_%d" % (s, q), len(topo.engines(cores[q], core)) // 2)
+
+    bank = [0, None, None]
+
+    def swap_pe(v, who, deps):
+        b = bank[0]
+        bank[0] = 1 - b
+        ps = T["ps%d" % b]
+        c, d = col(v, 0, who), col(v, 1, who)
+        kp = mm([(ps[:], PM, W[:, c:c + HB], True, True)], deps=list(deps) + [bank[1 + b], t_pm])
+        bank[1 + b] = acp(W[:, d:d + HB], ps[:], deps=[kp])
+        return bank[1 + b]
+
+    def swap_v(v, who, deps):
+        c, d = col(v, 0, who), col(v, 1, who)
+        cp(W[0:64, d:d + HB], W[64:128, c:c + HB], deps=deps)
+        return cp(W[64:128, d:d + HB], W[0:64, c:c + HB])
+
+    def swap_both(v, who, deps):
+        c, d, x = col(v, 0, who), col(v, 1, who), 192
+        cp(W[0:64, d:d + HB], W[64:128, c:c + HB], deps=deps)
+        kv = cp(W[64:128, d:d + x], W[0:64, c:c + x])
+        return kv, acp(W[64:128, d + x:d + HB], W[0:64, c + x:c + HB], deps=deps)
+
+    def weigh(t, R, deps):
+        c = col(t + 3, 0, mine[R])
+        return mm([(T.pa[:, 32 * R:32 * R + 32], T.wb[:, R * 144 + 15 - q:R * 144 + 143 - q],
+                    W[:, c + q:c + HB:16], q == 0, q == 15) for q in range(16)], deps=deps)
+
+    ai, who, zz, zm, zx, f1, jj = [T.xi[:, i * 64:(i + 1) * 64] for i in range(7)]
+    t1, base, v1, v2, ww = [T.xf[:, i * 64:(i + 1) * 64] for i in range(5)]
+
+    def chain_front(t, ka):
+        k = ts(ai, T.pa[:, 0:64], float(((S - t) % S) * VB), A.add, deps=[ka])
+        k = ts(who, ai, 3, A.bitwise_and, deps=[k])
+        ts(zz, ai, 2048 + 3, A.bitwise_and)
+        ts(T.hh[:, 0:64], who, float(mate), A.is_equal, deps=[k])
+        ts(T.hh[:, 64:128], who, float(pmate), A.is_equal)
+        ts(T.hh[:, 128:160], T.xi[:, 64:96], float(mine[1]), A.is_equal)
+        k = ts(T.hh[:, 160:192], T.xi[:, 96:128], float(mine[0]), A.is_equal)
+        ts(f1, ai, 3 * VB, A.bitwise_and)
+        wait("v", [k])
+        done("v", V.tensor_tensor_scan(T.sf[:], T.rst[:], T.hh[:], 0.0, A.mult, A.add))
+        return done("v", V.tensor_tensor_scan(T.sb[:, ::-1], T.rst[:], T.hh[:, ::-1], 0.0, A.mult, A.add))
+
+    def count(ks):
+        pc = T.pc[:, 0:192]
+        return mm([(pc, M3, T.hh[:], True, False), (pc, M1, T.sf[:], False, False), (pc, M2, T.sb[:], False, True)],
+                  deps=[ks])
+
+    def chain_back(t, kc):
+        kj = ts(jj, ai, 2, A.logical_shift_right, HB - 1, A.bitwise_and)
+        km = ts(zm, zz, 513.0, A.mult, flip, A.add)
+        tt(t1, f1, jj, A.add, deps=[kj])
+        k = ts(zx, zm, 2048 + 1024 + 512, A.bitwise_and, deps=[km])
+        kb = tt(base, t1, zx, A.add, deps=[k])
+        k2 = ts(T.uu[:], T.pc[:, 0:192], KH + CAP, A.is_gt, -65536.0, A.mult, deps=[kc])
+        tt(v1, T.uu[:, 0:64], T.uu[:, 64:128], A.add, deps=[k2])
+        k = tt(v2, T.uu[:, 128:192], base, A.add, deps=[kb])
+        k = tt(ww, v1, v2, A.add, deps=[k])
+        return ts(T.off[:], ww, float(Z + t * VB), A.add, 0.0, A.max, deps=[k])
+
+    def ahead(t, kk, deps):
+        R, o = kk // 2, (kk % 2) * 256
+        px_ = T["px%d" % kk][:, 0:256]
+        cprev, cold = col(t + 3, 0, mine[R]) + o, col(t, 0, mine[R]) + o
+        wait("p", deps)
+        PE.matmul(px_, T.gh[:, 2 * R * 128:(2 * R + 1) * 128], W[:, cprev:cprev + 256], True, False)
+        PE.matmul(px_, ID, W[:, cold:cold + 256], False, False)
+        PE.matmul(px_, ID, T.lift[:], False, False)
+
+    stores = [0]
+
+    def store(t, src, c, rows, deps):
+        s = t % S
+        wait("s", deps)
+        for p in range(2):
+            SY.dma_start(T.y[half(rows), s * SL + p * HB:s * SL + (p + 1) * HB],
+                         src[half(p), c:c + HB]).then_inc(T.sem.stored, 16)
+            stores[0] += 16
+
+    for s in order:
+        swap_pe(s, r, [arrived(s, r)])
+    t_w0 = stationaries(0, T.pkp, [("apk", len(topo.engines(cores[part], core)))])
+    weigh(0, 1, [t_w1])
+    ka = weigh(0, 0, [t_w0, arrived(3, part)])
+    swap_pe(3, part, [])
+    swap_v(3, mate, [arrived(3, mate)])
+    ks = chain_front(0, ka)
+    kc = count(ks)
+    k_off = chain_back(0, kc)
+    swap_v(3, pmate, [arrived(3, pmate)])
+    swap_pe(0, part, [arrived(0, part)])
+    for kk in range(4):
+        ahead(0, kk, [])
+    for s in order[1:]:
+        swap_v(s, mate, [arrived(s, mate)])
+        k_sv = swap_v(s, pmate, [arrived(s, pmate)])
+        if s != 0:
+            k_sa = swap_pe(s, part, [arrived(s, part)])
+
+    near = topo.engines(core, cores[mate])
+    far = topo.engines(core, cores[part])
+    n_back = len(topo.engines(cores[part], core))
+    for t in range(WAVES):
+        win = W[:, 0:Z + (t + 4) * VB]
+        ready = [k_off, k_sv, k_sa, t_z]
+        last = t == WAVES - 1
+
+        def gv(a, b):
+            return cp(T.ref[:, a:b], win.indirect(T.off[:, a // 16:b // 16]), deps=ready)
+
+        def ga(a, b):
+            return acp(T.ref[:, a:b], win.indirect(T.off[:, a // 16:b // 16]), deps=ready)
+
+        def finish(kk, deps):
+            R, o = kk // 2, (kk % 2) * 256
+            px_ = T["px%d" % kk][:, 0:256]
+            cs = slice(kk * 256, (kk + 1) * 256)
+            kh = mm([(px_, T.gh[:, (2 * R + 1) * 128:(2 * R + 2) * 128], T.ref[:, cs], False, True)], deps=deps)
+            wait("a", [kh])
+            kr = done("a", AC.activation(T.rnd[:, cs], px_, F.Identity, bias=-127.5))
+            c = col(t + 4, 0, mine[R]) + o
+            return tt(W[:, c:c + 256], px_, T.rnd[:, cs], A.subtract, deps=[kr])
+
+        if 2 <= t:
+            store(t - 1, W, col(t + 3, 0, r), M, [k_off])
+            store(t - 1, T.back, ((t - 1) % S) * HB, 1 - M, [("bk%d" % (t - 1), n_back)])
+        c0, c1 = col(t + 4, 0, mine[0]), col(t + 4, 0, mine[1])
+        back = RemoteDMATransfer(dst_ids=[dst(part)], dma_engine_mask=bits(far), remote_sem=T.sem["bk%d" % max(t, 1)],
+                                 src=W[:, c0:c0 + HB], dst=T.back[:, (t % S) * HB:(t % S + 1) * HB])
+        if last:
+            g0 = gv(0, 256)
+            g1 = ga(256, 416)
+            g2 = gv(416, 512)
+            finish(0, [g0])
+            n1 = finish(1, [g1, g2])
+            send([back], len(far), [n1])
+            g3 = gv(512, 768)
+            g4 = ga(768, 1024)
+            finish(2, [g3])
+            n3 = finish(3, [g4])
+            store(t, W, c1, M, [n3])
+            store(t, T.back, (t % S) * HB, 1 - M, [("bk%d" % t, n_back)])
+            break
+        g0 = gv(0, 256)
+        g2 = gv(640, 1024)
+        g1 = ga(256, 640)
+        need = [[g0], [g1], [g1, g2], [g2]]
+        new = [finish(kk, need[kk]) for kk in range(4)]
+        for b, c in enumerate((c0, c1)):
+            send([RemoteDMATransfer(dst_ids=[dst(mate)], dma_engine_mask=bits(near), remote_sem=T.sem["wv%d_%d" % (t, b)],
+                                    src=W[:, c:c + HB], dst=W[:, c:c + HB])], len(near), [new[2 * b + 1]])
+        if t >= 1:
+            send([back], len(far), [])
+        weigh(t + 1, 0, [new[1]])
+        ka = weigh(t + 1, 1, [new[3]])
+        ks = chain_front(t + 1, ka)
+        swap_pe(t + 4, mine[0], [])
+        swap_pe(t + 4, mine[1], [])
+        kc = count(ks)
+        k_off = chain_back(t + 1, kc)
+        for kk in range(4):
+            ahead(t + 1, kk, [])
+        n_in = len(topo.engines(cores[mate], core))
+        swap_pe(t + 4, theirs[0], [("wv%d_0" % t, n_in)])
+        k_sv, k_sa = swap_both(t + 4, theirs[1], [("wv%d_1" % t, n_in)])
+
+    wait("s", [("stored", stores[0])])
+    wait("g", [("sent", sent[0]), ("sv", Q["v"][2]), ("sa", Q["a"][2]), ("sp", Q["p"][2]), ("sg", Q["g"][2])])

@@ -8,33 +8,19 @@ KH = 1024.0
 LIFT = 129.0 * 256.0
 
 SCRATCH = {
-    "win": ("sbuf", [128, Z + 9 * VB], "bfloat16"),
-    "oth": ("sbuf", [128, S * HB], "bfloat16"),
-    "back": ("sbuf", [128, S * HB], "bfloat16"),
-    "pk": ("sbuf", [128, 272], "bfloat16"),
-    "pkp": ("sbuf", [128, 272], "bfloat16"),
-    "gh": ("sbuf", [128, 512], "bfloat16"),
-    "wc": ("sbuf", [128, 16], "float32"),
-    "wb": ("sbuf", [128, 288], "bfloat16"),
-    "ref": ("sbuf", [128, SL], "bfloat16"),
-    "rnd": ("sbuf", [128, SL], "bfloat16"),
-    "lift": ("sbuf", [128, 256], "bfloat16"),
-    "mats": ("sbuf", [128, 8 * 128], "bfloat16"),
-    "ci": ("sbuf", [128, 8], "int32"),
-    "cf": ("sbuf", [128, 8], "float32"),
-    "mi": ("sbuf", [128, 192], "int32"),
-    "mj": ("sbuf", [128, 320], "int32"),
-    "mf": ("sbuf", [128, 144], "float32"),
-    "rst": ("sbuf", [128, 192], "bfloat16"),
-    "xi": ("sbuf", [128, 7 * 64], "int32"),
-    "xf": ("sbuf", [128, 5 * 64], "float32"),
-    "hh": ("sbuf", [128, 192], "bfloat16"),
-    "sf": ("sbuf", [128, 192], "bfloat16"),
-    "sb": ("sbuf", [128, 192], "bfloat16"),
-    "uu": ("sbuf", [128, 192], "float32"),
-    "off": ("sbuf", [128, 64], "uint16"),
+    "win": ("sbuf", [128, Z + 9 * VB], "bfloat16"), "oth": ("sbuf", [128, S * HB], "bfloat16"),
+    "back": ("sbuf", [128, S * HB], "bfloat16"), "pk": ("sbuf", [128, 272], "bfloat16"),
+    "pkp": ("sbuf", [128, 272], "bfloat16"), "gh": ("sbuf", [128, 512], "bfloat16"),
+    "wc": ("sbuf", [128, 16], "float32"), "wb": ("sbuf", [128, 288], "bfloat16"),
+    "ref": ("sbuf", [128, SL], "bfloat16"), "rnd": ("sbuf", [128, SL], "bfloat16"),
+    "lift": ("sbuf", [128, 256], "bfloat16"), "mats": ("sbuf", [128, 8 * 128], "bfloat16"),
+    "ci": ("sbuf", [128, 8], "int32"), "cf": ("sbuf", [128, 12], "float32"), "mi": ("sbuf", [128, 256], "int32"),
+    "mj": ("sbuf", [128, 576], "int32"), "mf": ("sbuf", [128, 144], "float32"), "rst": ("sbuf", [128, 192], "bfloat16"),
+    "rs4": ("sbuf", [128, 256], "float32"), "xi": ("sbuf", [128, 7 * 64], "int32"), "xf": ("sbuf", [128, 64], "float32"),
+    "hh": ("sbuf", [128, 192], "bfloat16"), "sf": ("sbuf", [128, 192], "bfloat16"), "sb": ("sbuf", [128, 192], "bfloat16"),
+    "uu": ("sbuf", [128, 256], "float32"), "us": ("sbuf", [128, 256], "float32"), "off": ("sbuf", [128, 64], "uint16"),
 }
-for _n in ("px0", "px1", "px2", "px3", "pa", "pc", "ps0", "ps1"):
+for _n in ("px0", "px1", "px2", "px3", "px4", "px5", "pa", "pc"):
     SCRATCH[_n] = ("psum", [128, 512], "float32")
 SEMAPHORES = (["sv", "sa", "sp", "sg", "sent", "stored", "lpk", "apk"]
               + ["lw%d" % s for s in range(S)] + ["lo%d" % s for s in range(S)]
@@ -141,7 +127,7 @@ def rank_program(g, core, T, topo):
             dq.dma_start(W[half(p), c:c + HB], T.m[half(M), src]).then_inc(T.sem["lw%d" % s], 16)
 
     t_ci = done("g", g.iota(T.ci[:, 0:2], [[64, 2]], 0, 1))
-    t_mi = done("g", g.iota(T.mi[:], [[1, 192]], 0, 0))
+    t_mi = done("g", g.iota(T.mi[:], [[1, 256]], 0, 0))
     t_z = fill(W[:, 0:Z], 0.0)
     t_gh0 = fill(T.gh[:], 0.0)
     fill(T.lift[:], LIFT)
@@ -151,14 +137,15 @@ def rank_program(g, core, T, topo):
     k = ts(T.ci[:, 5:6], T.ci[:, 0:1], 6, A.logical_shift_right)
     k_mf = cp(T.mf[:], T.mi[:, 0:144], deps=[t_mi])
     ts(T.mj[:, 0:128], T.mi[:, 0:128], 4, A.logical_shift_right, 3, A.bitwise_and)
-    k_mj = ts(T.mj[:, 128:320], T.mi[:], 31, A.bitwise_and)
+    ts(T.mj[:, 320:576], T.mi[:], 3, A.bitwise_and)
+    k_mj = ts(T.mj[:, 128:320], T.mi[:, 0:192], 31, A.bitwise_and)
     k = cp(T.cf[:, 0:6], T.ci[:, 0:6], deps=[k])
     pf, px, pg, ph = T.cf[:, 0:1], T.cf[:, 2:3], T.cf[:, 3:4], T.cf[:, 5:6]
     ID, PM, M1, M2, M3, NS, LT, KI = [T.mats[:, i * 128:(i + 1) * 128] for i in range(8)]
     t_pm = ts(PM, T.mf[:, 0:128], px, A.is_equal, deps=[k, k_mf])
-    ts(T.cf[:, 6:7], T.cf[:, 4:5], 15.0, A.add)
+    ts(T.cf[:, 8:9], T.cf[:, 4:5], 15.0, A.add)
     k_cf = ts(T.cf[:, 7:8], ph, 2048.0, A.mult)
-    p15, flip = T.cf[:, 6:7], T.cf[:, 7:8]
+    p15, flip = T.cf[:, 8:9], T.cf[:, 7:8]
 
     def stationaries(R, pk, deps):
         for p in range(2):
@@ -175,6 +162,7 @@ def rank_program(g, core, T, topo):
     ts(LT, T.mf[:, 0:128], pf, A.is_lt)
     ts(KI, T.mf[:, 0:128], pf, A.is_equal, KH, A.mult)
     fill(M2, 0.0)
+    ts(T.rs4[:], T.mj[:, 320:576], 0.0, A.is_gt)
     k = ts(T.rst[:], T.mj[:, 128:320], 0.0, A.is_gt)
     k = tt(LT, LT, NS, A.mult, deps=[k])
     cp(T.mats[0:64, 3 * 128 + 64:4 * 128], T.mats[0:64, 2 * 128 + 64:3 * 128])
@@ -203,27 +191,19 @@ def rank_program(g, core, T, topo):
             return ("lw%d" % s, 32)
         return ("in%d_%d" % (s, q), len(topo.engines(cores[q], core)) // 2)
 
-    bank = [0, None, None]
+    freed = {}
 
-    def swap_pe(v, who, deps):
-        b = bank[0]
-        bank[0] = 1 - b
-        ps = T["ps%d" % b]
+    def swap_pe(b, v, who, deps):
+        ps = T["px%d" % b]
         c, d = col(v, 0, who), col(v, 1, who)
-        kp = mm([(ps[:], PM, W[:, c:c + HB], True, True)], deps=list(deps) + [bank[1 + b], t_pm])
-        bank[1 + b] = acp(W[:, d:d + HB], ps[:], deps=[kp])
-        return bank[1 + b]
+        kp = mm([(ps[:], PM, W[:, c:c + HB], True, True)], deps=list(deps) + [freed.get(b), t_pm])
+        freed[b] = acp(W[:, d:d + HB], ps[:], deps=[kp])
+        return freed[b]
 
-    def swap_v(v, who, deps):
+    def swap(op, v, who, deps):
         c, d = col(v, 0, who), col(v, 1, who)
-        cp(W[0:64, d:d + HB], W[64:128, c:c + HB], deps=deps)
-        return cp(W[64:128, d:d + HB], W[0:64, c:c + HB])
-
-    def swap_both(v, who, deps):
-        c, d, x = col(v, 0, who), col(v, 1, who), 192
-        cp(W[0:64, d:d + HB], W[64:128, c:c + HB], deps=deps)
-        kv = cp(W[64:128, d:d + x], W[0:64, c:c + x])
-        return kv, acp(W[64:128, d + x:d + HB], W[0:64, c + x:c + HB], deps=deps)
+        op(W[half(0), d:d + HB], W[half(1), c:c + HB], deps=deps)
+        return op(W[half(1), d:d + HB], W[half(0), c:c + HB])
 
     def weigh(t, R, deps):
         c = col(t + 3, 0, mine[R])
@@ -231,46 +211,54 @@ def rank_program(g, core, T, topo):
                     W[:, c + q:c + HB:16], q == 0, q == 15) for q in range(16)], deps=deps)
 
     ai, who, zz, zm, zx, f1, jj = [T.xi[:, i * 64:(i + 1) * 64] for i in range(7)]
-    t1, base, v1, v2, ww = [T.xf[:, i * 64:(i + 1) * 64] for i in range(5)]
+    t1 = T.xf[:]
+
+    def scan(out, keep, data):
+        return done("v", V.tensor_tensor_scan(out, keep, data, 0.0, A.mult, A.add))
 
     def chain_front(t, ka):
         k = ts(ai, T.pa[:, 0:64], float(((S - t) % S) * VB), A.add, deps=[ka])
         k = ts(who, ai, 3, A.bitwise_and, deps=[k])
         ts(zz, ai, 2048 + 3, A.bitwise_and)
+        k0 = ts(f1, ai, 3 * VB, A.bitwise_and)
         ts(T.hh[:, 0:64], who, float(mate), A.is_equal, deps=[k])
         ts(T.hh[:, 64:128], who, float(pmate), A.is_equal)
         ts(T.hh[:, 128:160], T.xi[:, 64:96], float(mine[1]), A.is_equal)
         k = ts(T.hh[:, 160:192], T.xi[:, 96:128], float(mine[0]), A.is_equal)
-        ts(f1, ai, 3 * VB, A.bitwise_and)
+        ts(jj, ai, 2, A.logical_shift_right, HB - 1, A.bitwise_and)
+        km = ts(zm, zz, 513.0, A.mult, flip, A.add, deps=[k0])
         wait("v", [k])
-        done("v", V.tensor_tensor_scan(T.sf[:], T.rst[:], T.hh[:], 0.0, A.mult, A.add))
-        return done("v", V.tensor_tensor_scan(T.sb[:, ::-1], T.rst[:], T.hh[:, ::-1], 0.0, A.mult, A.add))
+        scan(T.sf[:], T.rst[:], T.hh[:])
+        return scan(T.sb[:, ::-1], T.rst[:], T.hh[:, ::-1]), km
 
     def count(ks):
         pc = T.pc[:, 0:192]
         return mm([(pc, M3, T.hh[:], True, False), (pc, M1, T.sf[:], False, False), (pc, M2, T.sb[:], False, True)],
                   deps=[ks])
 
-    def chain_back(t, kc):
-        kj = ts(jj, ai, 2, A.logical_shift_right, HB - 1, A.bitwise_and)
-        km = ts(zm, zz, 513.0, A.mult, flip, A.add)
-        tt(t1, f1, jj, A.add, deps=[kj])
-        k = ts(zx, zm, 2048 + 1024 + 512, A.bitwise_and, deps=[km])
-        kb = tt(base, t1, zx, A.add, deps=[k])
-        k2 = ts(T.uu[:], T.pc[:, 0:192], KH + CAP, A.is_gt, -65536.0, A.mult, deps=[kc])
-        tt(v1, T.uu[:, 0:64], T.uu[:, 64:128], A.add, deps=[k2])
-        k = tt(v2, T.uu[:, 128:192], base, A.add, deps=[kb])
-        k = tt(ww, v1, v2, A.add, deps=[k])
-        return ts(T.off[:], ww, float(Z + t * VB), A.add, 0.0, A.max, deps=[k])
+    def chain_back(t, kc, km):
+        ts(zx, zm, 2048 + 1024 + 512, A.bitwise_and, deps=[km])
+        k = tt(t1, f1, jj, A.add)
+        tt(T.uu[:, 3:256:4], t1, zx, A.add, deps=[k])
+        for i in range(3):
+            k = ts(T.uu[:, i:256:4], T.pc[:, 64 * i:64 * i + 64], KH + CAP, A.is_gt, -65536.0, A.mult, deps=[kc])
+        wait("v", [k])
+        k = scan(T.us[:], T.rs4[:], T.uu[:])
+        return ts(T.off[:], T.us[:, 3:256:4], float(Z + t * VB), A.add, 0.0, A.max, deps=[k])
 
-    def ahead(t, kk, deps):
+    def acc(t, kk):
+        return T["px%d" % ((4 * t + kk) % 6)][:, 0:256]
+
+    def ahead(t, kk, what, deps=()):
         R, o = kk // 2, (kk % 2) * 256
-        px_ = T["px%d" % kk][:, 0:256]
         cprev, cold = col(t + 3, 0, mine[R]) + o, col(t, 0, mine[R]) + o
-        wait("p", deps)
-        PE.matmul(px_, T.gh[:, 2 * R * 128:(2 * R + 1) * 128], W[:, cprev:cprev + 256], True, False)
-        PE.matmul(px_, ID, W[:, cold:cold + 256], False, False)
-        PE.matmul(px_, ID, T.lift[:], False, False)
+        wait("p", list(deps) + [freed.get((4 * t + kk) % 6)])
+        if "l" in what:
+            PE.matmul(acc(t, kk), ID, T.lift[:], True, False)
+        if "o" in what:
+            PE.matmul(acc(t, kk), ID, W[:, cold:cold + 256], False, False)
+        if "g" in what:
+            PE.matmul(acc(t, kk), T.gh[:, 2 * R * 128:(2 * R + 1) * 128], W[:, cprev:cprev + 256], False, False)
 
     stores = [0]
 
@@ -282,29 +270,33 @@ def rank_program(g, core, T, topo):
                          src[half(p), c:c + HB]).then_inc(T.sem.stored, 16)
             stores[0] += 16
 
-    for s in order:
-        swap_pe(s, r, [arrived(s, r)])
+    for n, s in enumerate(order):
+        swap_pe(5 - n % 2, s, r, [arrived(s, r)])
     t_w0 = stationaries(0, T.pkp, [("apk", len(topo.engines(cores[part], core)))])
     weigh(0, 1, [t_w1])
+    ahead(0, 2, "log")
+    ahead(0, 3, "log")
     ka = weigh(0, 0, [t_w0, arrived(3, part)])
-    swap_pe(3, part, [])
-    swap_v(3, mate, [arrived(3, mate)])
-    ks = chain_front(0, ka)
+    swap_pe(5, 3, part, [])
+    swap(cp, 3, mate, [arrived(3, mate)])
+    ks, km = chain_front(0, ka)
+    ahead(0, 0, "lg")
     kc = count(ks)
-    k_off = chain_back(0, kc)
-    swap_v(3, pmate, [arrived(3, pmate)])
-    swap_pe(0, part, [arrived(0, part)])
-    for kk in range(4):
-        ahead(0, kk, [])
-    for s in order[1:]:
-        swap_v(s, mate, [arrived(s, mate)])
-        k_sv = swap_v(s, pmate, [arrived(s, pmate)])
-        if s != 0:
-            k_sa = swap_pe(s, part, [arrived(s, part)])
+    k_off = chain_back(0, kc, km)
+    swap(cp, 3, pmate, [arrived(3, pmate)])
+    ahead(0, 1, "lg")
+    for n, s in enumerate(order[1:]):
+        swap(cp, s, mate, [arrived(s, mate)])
+        k_sv = swap(cp, s, pmate, [arrived(s, pmate)])
+        k_sa = swap_pe(5 - n % 2, s, part, [arrived(s, part)])
+        if n == 0:
+            ahead(0, 0, "o")
+            ahead(0, 1, "o")
 
     near = topo.engines(core, cores[mate])
     far = topo.engines(core, cores[part])
     n_back = len(topo.engines(cores[part], core))
+    n_in = len(topo.engines(cores[mate], core))
     for t in range(WAVES):
         win = W[:, 0:Z + (t + 4) * VB]
         ready = [k_off, k_sv, k_sa, t_z]
@@ -318,7 +310,7 @@ def rank_program(g, core, T, topo):
 
         def finish(kk, deps):
             R, o = kk // 2, (kk % 2) * 256
-            px_ = T["px%d" % kk][:, 0:256]
+            px_ = acc(t, kk)
             cs = slice(kk * 256, (kk + 1) * 256)
             kh = mm([(px_, T.gh[:, (2 * R + 1) * 128:(2 * R + 2) * 128], T.ref[:, cs], False, True)], deps=deps)
             wait("a", [kh])
@@ -330,16 +322,19 @@ def rank_program(g, core, T, topo):
             store(t - 1, W, col(t + 3, 0, r), M, [k_off])
             store(t - 1, T.back, ((t - 1) % S) * HB, 1 - M, [("bk%d" % (t - 1), n_back)])
         c0, c1 = col(t + 4, 0, mine[0]), col(t + 4, 0, mine[1])
-        back = RemoteDMATransfer(dst_ids=[dst(part)], dma_engine_mask=bits(far), remote_sem=T.sem["bk%d" % max(t, 1)],
-                                 src=W[:, c0:c0 + HB], dst=T.back[:, (t % S) * HB:(t % S + 1) * HB])
+
+        def back(deps):
+            o = (t % S) * HB
+            send([RemoteDMATransfer(dst_ids=[dst(part)], dma_engine_mask=bits(far), remote_sem=T.sem["bk%d" % t],
+                                    src=W[:, c0:c0 + HB], dst=T.back[:, o:o + HB])], len(far), deps)
+
         if last:
             g0 = gv(0, 256)
-            g1 = ga(256, 416)
-            g2 = gv(416, 512)
-            finish(0, [g0])
-            n1 = finish(1, [g1, g2])
-            send([back], len(far), [n1])
+            g1 = ga(256, 512)
             g3 = gv(512, 768)
+            finish(0, [g0])
+            n1 = finish(1, [g1])
+            back([n1])
             g4 = ga(768, 1024)
             finish(2, [g3])
             n3 = finish(3, [g4])
@@ -349,25 +344,28 @@ def rank_program(g, core, T, topo):
         g0 = gv(0, 256)
         g2 = gv(640, 1024)
         g1 = ga(256, 640)
-        need = [[g0], [g1], [g1, g2], [g2]]
-        new = [finish(kk, need[kk]) for kk in range(4)]
+        new = [finish(0, [g0]), finish(1, [g1])]
+        ahead(t + 1, 0, "lo")
+        new += [finish(2, [g1, g2]), finish(3, [g2])]
+        ahead(t + 1, 1, "lo")
         for b, c in enumerate((c0, c1)):
             send([RemoteDMATransfer(dst_ids=[dst(mate)], dma_engine_mask=bits(near), remote_sem=T.sem["wv%d_%d" % (t, b)],
                                     src=W[:, c:c + HB], dst=W[:, c:c + HB])], len(near), [new[2 * b + 1]])
         if t >= 1:
-            send([back], len(far), [])
+            back([])
         weigh(t + 1, 0, [new[1]])
         ka = weigh(t + 1, 1, [new[3]])
-        ks = chain_front(t + 1, ka)
-        swap_pe(t + 4, mine[0], [])
-        swap_pe(t + 4, mine[1], [])
+        swap(acp, t + 4, mine[0], [new[1]])
+        swap_pe((4 * t + 2) % 6, t + 4, mine[1], [])
+        ks, km = chain_front(t + 1, ka)
+        ahead(t + 1, 0, "g")
+        ahead(t + 1, 1, "g")
+        ahead(t + 1, 2, "log")
         kc = count(ks)
-        k_off = chain_back(t + 1, kc)
-        for kk in range(4):
-            ahead(t + 1, kk, [])
-        n_in = len(topo.engines(cores[mate], core))
-        swap_pe(t + 4, theirs[0], [("wv%d_0" % t, n_in)])
-        k_sv, k_sa = swap_both(t + 4, theirs[1], [("wv%d_1" % t, n_in)])
+        k_off = chain_back(t + 1, kc, km)
+        swap_pe((4 * t + 3) % 6, t + 4, theirs[0], [("wv%d_0" % t, n_in)])
+        ahead(t + 1, 3, "log")
+        k_sa = swap_pe((4 * t + 2) % 6, t + 4, theirs[1], [("wv%d_1" % t, n_in)])
 
     wait("s", [("stored", stores[0])])
     wait("g", [("sent", sent[0]), ("sv", Q["v"][2]), ("sa", Q["a"][2]), ("sp", Q["p"][2]), ("sg", Q["g"][2])])

@@ -4,8 +4,10 @@ from concourse.mybir import AluOpType as A, ActivationFunctionType as F
 S, SL, HB, WAVES, CAP = 4, 1024, 512, 5, 320
 Z = 16
 VB = 4096
-KH = 1024.0
+KH = float(SL - CAP)
+STEP = 131072.0
 LIFT = 129.0 * 256.0
+OPT = {"last": "split", "gv": 896, "sendsw": 1, "x": 320}
 
 SCRATCH = {
     "win": ("sbuf", [128, Z + 9 * VB], "bfloat16"), "oth": ("sbuf", [128, S * HB], "bfloat16"),
@@ -13,10 +15,10 @@ SCRATCH = {
     "pkp": ("sbuf", [128, 272], "bfloat16"), "gh": ("sbuf", [128, 512], "bfloat16"),
     "wc": ("sbuf", [128, 16], "float32"), "wb": ("sbuf", [128, 288], "bfloat16"),
     "ref": ("sbuf", [128, SL], "bfloat16"), "rnd": ("sbuf", [128, SL], "bfloat16"),
-    "lift": ("sbuf", [128, 256], "bfloat16"), "mats": ("sbuf", [128, 8 * 128], "bfloat16"),
-    "ci": ("sbuf", [128, 8], "int32"), "cf": ("sbuf", [128, 12], "float32"), "mi": ("sbuf", [128, 256], "int32"),
+    "lift": ("sbuf", [128, 256], "bfloat16"), "mats": ("sbuf", [128, 9 * 128], "bfloat16"),
+    "ci": ("sbuf", [128, 8], "int32"), "cf": ("sbuf", [128, 16], "float32"), "mi": ("sbuf", [128, 256], "int32"),
     "mj": ("sbuf", [128, 576], "int32"), "mf": ("sbuf", [128, 144], "float32"), "rst": ("sbuf", [128, 192], "bfloat16"),
-    "rs4": ("sbuf", [128, 256], "float32"), "xi": ("sbuf", [128, 7 * 64], "int32"), "xf": ("sbuf", [128, 64], "float32"),
+    "rs4": ("sbuf", [128, 256], "bfloat16"), "xi": ("sbuf", [128, 5 * 64], "int32"),
     "hh": ("sbuf", [128, 192], "bfloat16"), "sf": ("sbuf", [128, 192], "bfloat16"), "sb": ("sbuf", [128, 192], "bfloat16"),
     "uu": ("sbuf", [128, 256], "float32"), "us": ("sbuf", [128, 256], "float32"), "off": ("sbuf", [128, 64], "uint16"),
 }
@@ -25,7 +27,7 @@ for _n in ("px0", "px1", "px2", "px3", "px4", "px5", "pa", "pc"):
 SEMAPHORES = (["sv", "sa", "sp", "sg", "sent", "stored", "lpk", "apk"]
               + ["lw%d" % s for s in range(S)] + ["lo%d" % s for s in range(S)]
               + ["in%d_%d" % (s, r) for s in range(S) for r in range(4)]
-              + ["wv%d_%d" % (t, b) for t in range(WAVES - 1) for b in range(2)]
+              + ["wv%d_%d" % (t, b) for t in range(WAVES - 1) for b in range(3)]
               + ["bk%d" % t for t in range(1, WAVES)])
 
 
@@ -113,7 +115,7 @@ def rank_program(g, core, T, topo):
     order = [3, 0, 1, 2]
     t_pad = fill(T.pk[:, 256:272], 0.0)
     AC.dma_start(T.pk[:, 0:128], T.gm[:]).then_inc(T.sem.lpk, 16)
-    AC.dma_start(T.pk[:, 128:256], T.hm[:]).then_inc(T.sem.lpk, 16)
+    SY.dma_start(T.pk[:, 128:256], T.hm[:]).then_inc(T.sem.lpk, 16)
     wait("a", [t_pad])
     AC.dma_start(T.pk[:, 256:257], T.kw[:]).then_inc(T.sem.lpk, 16)
     for n, s in enumerate(order):
@@ -131,6 +133,7 @@ def rank_program(g, core, T, topo):
     t_z = fill(W[:, 0:Z], 0.0)
     t_gh0 = fill(T.gh[:], 0.0)
     fill(T.lift[:], LIFT)
+    fill(T.uu[:], 8192.0 * STEP)
     ts(T.ci[:, 2:3], T.ci[:, 1:2], 127, A.bitwise_and, deps=[t_ci])
     ts(T.ci[:, 3:4], T.ci[:, 0:1], 4, A.logical_shift_right, 3, A.bitwise_and)
     ts(T.ci[:, 4:5], T.ci[:, 0:1], 112, A.bitwise_and)
@@ -141,11 +144,14 @@ def rank_program(g, core, T, topo):
     k_mj = ts(T.mj[:, 128:320], T.mi[:, 0:192], 31, A.bitwise_and)
     k = cp(T.cf[:, 0:6], T.ci[:, 0:6], deps=[k])
     pf, px, pg, ph = T.cf[:, 0:1], T.cf[:, 2:3], T.cf[:, 3:4], T.cf[:, 5:6]
-    ID, PM, M1, M2, M3, NS, LT, KI = [T.mats[:, i * 128:(i + 1) * 128] for i in range(8)]
+    ID, PM, M1, M2, M3, NS, LT, KI, K0 = [T.mats[:, i * 128:(i + 1) * 128] for i in range(9)]
     t_pm = ts(PM, T.mf[:, 0:128], px, A.is_equal, deps=[k, k_mf])
     ts(T.cf[:, 8:9], T.cf[:, 4:5], 15.0, A.add)
+    ts(T.cf[:, 9:10], ph, -2.0, A.mult, 1.0, A.add)
+    ts(T.cf[:, 10:11], pf, 0.0, A.is_equal, SL * STEP, A.mult)
+    ts(T.cf[:, 11:12], pf, 1.0, A.is_equal, 0.5 * STEP, A.mult)
     k_cf = ts(T.cf[:, 7:8], ph, 2048.0, A.mult)
-    p15, flip = T.cf[:, 8:9], T.cf[:, 7:8]
+    p15, flip, sign = T.cf[:, 8:9], T.cf[:, 7:8], T.cf[:, 9:10]
 
     def stationaries(R, pk, deps):
         for p in range(2):
@@ -157,13 +163,15 @@ def rank_program(g, core, T, topo):
                   deps=[k2, k_cf])
 
     ts(ID, T.mf[:, 0:128], pf, A.is_equal)
-    ts(M1, T.mj[:, 0:128], pg, A.is_equal, deps=[k_mj])
-    ts(NS, T.mj[:, 0:128], pg, A.is_equal, -1.0, A.mult)
+    ts(M1, T.mj[:, 0:128], pg, A.is_equal, -STEP, A.mult, deps=[k_mj])
+    ts(NS, T.mj[:, 0:128], pg, A.is_equal, STEP, A.mult)
     ts(LT, T.mf[:, 0:128], pf, A.is_lt)
-    ts(KI, T.mf[:, 0:128], pf, A.is_equal, KH, A.mult)
+    ts(KI, T.mf[:, 0:128], pf, A.is_equal, -KH * STEP, A.mult)
+    k0 = tt(T.cf[:, 12:13], T.cf[:, 10:11], T.cf[:, 11:12], A.add, deps=[k_cf])
     fill(M2, 0.0)
     ts(T.rs4[:], T.mj[:, 320:576], 0.0, A.is_gt)
     k = ts(T.rst[:], T.mj[:, 128:320], 0.0, A.is_gt)
+    ts(K0, T.mf[:, 0:128], -1.0, A.is_gt, T.cf[:, 12:13], A.mult, deps=[k0])
     k = tt(LT, LT, NS, A.mult, deps=[k])
     cp(T.mats[0:64, 3 * 128 + 64:4 * 128], T.mats[0:64, 2 * 128 + 64:3 * 128])
     fill(T.mats[64:128, 2 * 128:2 * 128 + 64], 0.0)
@@ -200,51 +208,55 @@ def rank_program(g, core, T, topo):
         freed[b] = acp(W[:, d:d + HB], ps[:], deps=[kp])
         return freed[b]
 
-    def swap(op, v, who, deps):
+    def swap(op, v, who, deps, o=0, n=HB):
+        c, d = col(v, 0, who) + o, col(v, 1, who) + o
+        op(W[half(0), d:d + n], W[half(1), c:c + n], deps=deps)
+        return op(W[half(1), d:d + n], W[half(0), c:c + n])
+
+    def swap_both(v, who, deps, x=160):
         c, d = col(v, 0, who), col(v, 1, who)
-        op(W[half(0), d:d + HB], W[half(1), c:c + HB], deps=deps)
-        return op(W[half(1), d:d + HB], W[half(0), c:c + HB])
+        ka = acp(W[half(1), d + x:d + HB], W[half(0), c + x:c + HB], deps=deps)
+        cp(W[half(0), d:d + HB], W[half(1), c:c + HB], deps=deps)
+        return cp(W[half(1), d:d + x], W[half(0), c:c + x]), ka
 
     def weigh(t, R, deps):
         c = col(t + 3, 0, mine[R])
         return mm([(T.pa[:, 32 * R:32 * R + 32], T.wb[:, R * 144 + 15 - q:R * 144 + 143 - q],
                     W[:, c + q:c + HB:16], q == 0, q == 15) for q in range(16)], deps=deps)
 
-    ai, who, zz, zm, zx, f1, jj = [T.xi[:, i * 64:(i + 1) * 64] for i in range(7)]
-    t1 = T.xf[:]
-
-    def scan(out, keep, data):
-        return done("v", V.tensor_tensor_scan(out, keep, data, 0.0, A.mult, A.add))
+    ai, who, hb, f1, jj = [T.xi[:, i * 64:(i + 1) * 64] for i in range(5)]
 
     def chain_front(t, ka):
         k = ts(ai, T.pa[:, 0:64], float(((S - t) % S) * VB), A.add, deps=[ka])
         k = ts(who, ai, 3, A.bitwise_and, deps=[k])
-        ts(zz, ai, 2048 + 3, A.bitwise_and)
-        k0 = ts(f1, ai, 3 * VB, A.bitwise_and)
+        ts(hb, ai, 2048, A.bitwise_and)
         ts(T.hh[:, 0:64], who, float(mate), A.is_equal, deps=[k])
         ts(T.hh[:, 64:128], who, float(pmate), A.is_equal)
         ts(T.hh[:, 128:160], T.xi[:, 64:96], float(mine[1]), A.is_equal)
-        k = ts(T.hh[:, 160:192], T.xi[:, 96:128], float(mine[0]), A.is_equal)
+        kh = ts(T.hh[:, 160:192], T.xi[:, 96:128], float(mine[0]), A.is_equal)
         ts(jj, ai, 2, A.logical_shift_right, HB - 1, A.bitwise_and)
-        km = ts(zm, zz, 513.0, A.mult, flip, A.add, deps=[k0])
-        wait("v", [k])
-        scan(T.sf[:], T.rst[:], T.hh[:])
-        return scan(T.sb[:, ::-1], T.rst[:], T.hh[:, ::-1]), km
+        wait("v", [kh])
+        kf = done("v", V.tensor_tensor_scan(T.sf[:], T.rst[:], T.hh[:], 0.0, A.mult, A.add))
+        kb = done("v", V.tensor_tensor_scan(T.sb[:, ::-1], T.rst[:], T.hh[:, ::-1], 0.0, A.mult, A.add))
+        return kh, kf, kb
 
-    def count(ks):
-        pc = T.pc[:, 0:192]
-        return mm([(pc, M3, T.hh[:], True, False), (pc, M1, T.sf[:], False, False), (pc, M2, T.sb[:], False, True)],
-                  deps=[ks])
+    def open_count(deps):
+        return mm([(T.pc[:, 0:256], K0, T.rs4[:], True, False)], deps=deps)
 
-    def chain_back(t, kc, km):
-        ts(zx, zm, 2048 + 1024 + 512, A.bitwise_and, deps=[km])
-        k = tt(t1, f1, jj, A.add)
-        tt(T.uu[:, 3:256:4], t1, zx, A.add, deps=[k])
-        for i in range(3):
-            k = ts(T.uu[:, i:256:4], T.pc[:, 64 * i:64 * i + 64], KH + CAP, A.is_gt, -65536.0, A.mult, deps=[kc])
-        wait("v", [k])
-        k = scan(T.us[:], T.rs4[:], T.uu[:])
-        return ts(T.off[:], T.us[:, 3:256:4], float(Z + t * VB), A.add, 0.0, A.max, deps=[k])
+    def count(ko, ks):
+        for n, (mat, src) in enumerate(((M3, T.hh), (M1, T.sf), (M2, T.sb))):
+            kc = mm([(T.pc[:, 1 + i:256:4], mat, src[:, 64 * i:64 * i + 64], False, n == 2 and i == 2)
+                     for i in range(3)], deps=[ko, ks[n]])
+        return kc
+
+    def chain_back(t, kc):
+        k = ts(f1, ai, 3 * VB, A.bitwise_and)
+        ts(T.uu[:, 2:256:4], who, float(HB), A.mult)
+        ts(T.uu[:, 3:256:4], hb, sign, A.mult, flip, A.add)
+        k = tt(T.uu[:, 1:256:4], f1, jj, A.add, deps=[k])
+        wait("v", [k, kc])
+        k = done("v", V.tensor_tensor_scan(T.us[:], T.uu[:], T.pc[:, 0:256], 0.0, A.add, A.min))
+        return ts(T.off[:], T.us[:, 3:256:4], float(Z + t * VB), A.add, 0.0, A.max, deps=[k]), k
 
     def acc(t, kk):
         return T["px%d" % ((4 * t + kk) % 6)][:, 0:256]
@@ -270,6 +282,7 @@ def rank_program(g, core, T, topo):
                          src[half(p), c:c + HB]).then_inc(T.sem.stored, 16)
             stores[0] += 16
 
+    ko = open_count([t_w1])
     for n, s in enumerate(order):
         swap_pe(5 - n % 2, s, r, [arrived(s, r)])
     t_w0 = stationaries(0, T.pkp, [("apk", len(topo.engines(cores[part], core)))])
@@ -279,16 +292,19 @@ def rank_program(g, core, T, topo):
     ka = weigh(0, 0, [t_w0, arrived(3, part)])
     swap_pe(5, 3, part, [])
     swap(cp, 3, mate, [arrived(3, mate)])
-    ks, km = chain_front(0, ka)
+    ks = chain_front(0, ka)
     ahead(0, 0, "lg")
-    kc = count(ks)
-    k_off = chain_back(0, kc, km)
+    kc = count(ko, ks)
+    k_off, k_us = chain_back(0, kc)
     swap(cp, 3, pmate, [arrived(3, pmate)])
     ahead(0, 1, "lg")
     for n, s in enumerate(order[1:]):
         swap(cp, s, mate, [arrived(s, mate)])
-        k_sv = swap(cp, s, pmate, [arrived(s, pmate)])
         k_sa = swap_pe(5 - n % 2, s, part, [arrived(s, part)])
+        if n < 2:
+            swap(cp, s, pmate, [arrived(s, pmate)])
+        else:
+            k_sv, k_sa = swap_both(s, pmate, [arrived(s, pmate)])
         if n == 0:
             ahead(0, 0, "o")
             ahead(0, 1, "o")
@@ -316,11 +332,13 @@ def rank_program(g, core, T, topo):
             wait("a", [kh])
             kr = done("a", AC.activation(T.rnd[:, cs], px_, F.Identity, bias=-127.5))
             c = col(t + 4, 0, mine[R]) + o
-            return tt(W[:, c:c + 256], px_, T.rnd[:, cs], A.subtract, deps=[kr])
+            freed[(4 * t + kk) % 6] = tt(W[:, c:c + 256], px_, T.rnd[:, cs], A.subtract, deps=[kr])
+            return freed[(4 * t + kk) % 6]
 
         if 2 <= t:
             store(t - 1, W, col(t + 3, 0, r), M, [k_off])
-            store(t - 1, T.back, ((t - 1) % S) * HB, 1 - M, [("bk%d" % (t - 1), n_back)])
+            if last:
+                store(t - 1, T.back, ((t - 1) % S) * HB, 1 - M, [("bk%d" % (t - 1), n_back)])
         c0, c1 = col(t + 4, 0, mine[0]), col(t + 4, 0, mine[1])
 
         def back(deps):
@@ -341,31 +359,44 @@ def rank_program(g, core, T, topo):
             store(t, W, c1, M, [n3])
             store(t, T.back, (t % S) * HB, 1 - M, [("bk%d" % t, n_back)])
             break
+        x = OPT["gv"]
         g0 = gv(0, 256)
-        g2 = gv(640, 1024)
-        g1 = ga(256, 640)
-        new = [finish(0, [g0]), finish(1, [g1])]
+        g1 = ga(256, 512)
+        g2 = gv(512, 768)
+        g3 = gv(768, x)
+        g4 = ga(x, 1024)
+        ko = open_count([k_us])
         ahead(t + 1, 0, "lo")
-        new += [finish(2, [g1, g2]), finish(3, [g2])]
+        new = [finish(0, [g0]), finish(1, [g1])]
         ahead(t + 1, 1, "lo")
-        for b, c in enumerate((c0, c1)):
-            send([RemoteDMATransfer(dst_ids=[dst(mate)], dma_engine_mask=bits(near), remote_sem=T.sem["wv%d_%d" % (t, b)],
-                                    src=W[:, c:c + HB], dst=W[:, c:c + HB])], len(near), [new[2 * b + 1]])
-        if t >= 1:
-            back([])
+        new += [finish(2, [g2]), finish(3, [g3, g4])]
+        k_own = swap(cp, t + 4, mine[1], [new[3]])
+        for b, (c, kk) in enumerate(((c0, new[1]), (c1, new[3]), (col(t + 4, 1, mine[1]), k_own))[:2 + OPT["sendsw"]]):
+            send([RemoteDMATransfer(dst_ids=[dst(mate)], dma_engine_mask=bits(near), remote_sem=T.sem["wv%d_%d" % (t, min(b, 1))],
+                                    src=W[:, c:c + HB], dst=W[:, c:c + HB])], len(near), [kk])
         weigh(t + 1, 0, [new[1]])
         ka = weigh(t + 1, 1, [new[3]])
+        left = ("sent", sent[0])
+        if t >= 2:
+            store(t - 1, T.back, ((t - 1) % S) * HB, 1 - M, [("bk%d" % (t - 1), n_back), left])
+        if t >= 1:
+            back([left])
         swap(acp, t + 4, mine[0], [new[1]])
-        swap_pe((4 * t + 2) % 6, t + 4, mine[1], [])
-        ks, km = chain_front(t + 1, ka)
+        ks = chain_front(t + 1, ka)
         ahead(t + 1, 0, "g")
         ahead(t + 1, 1, "g")
-        ahead(t + 1, 2, "log")
-        kc = count(ks)
-        k_off = chain_back(t + 1, kc, km)
-        swap_pe((4 * t + 3) % 6, t + 4, theirs[0], [("wv%d_0" % t, n_in)])
+        ahead(t + 1, 2, "lo")
+        kc = count(ko, ks)
+        k_off, k_us = chain_back(t + 1, kc)
+        k_sa = swap(acp, t + 4, theirs[0], [("wv%d_0" % t, n_in)])
+        ahead(t + 1, 2, "g")
         ahead(t + 1, 3, "log")
-        k_sa = swap_pe((4 * t + 2) % 6, t + 4, theirs[1], [("wv%d_1" % t, n_in)])
+        if OPT["sendsw"]:
+            k_sv = ("wv%d_1" % t, 2 * n_in)
+        elif OPT["last"] == "split":
+            k_sv, k_sa = swap_both(t + 4, theirs[1], [("wv%d_1" % t, n_in)], OPT["x"])
+        else:
+            k_sa = swap_pe((4 * t + 2) % 6, t + 4, theirs[1], [("wv%d_1" % t, n_in)])
 
     wait("s", [("stored", stores[0])])
     wait("g", [("sent", sent[0]), ("sv", Q["v"][2]), ("sa", Q["a"][2]), ("sp", Q["p"][2]), ("sg", Q["g"][2])])

@@ -20,6 +20,7 @@ SCRATCH = {
     "mj": ("sbuf", [128, 576], "int32"), "mf": ("sbuf", [128, 144], "float32"), "rst": ("sbuf", [128, 192], "bfloat16"),
     "rs4": ("sbuf", [128, 256], "bfloat16"), "xi": ("sbuf", [128, 5 * 64], "int32"),
     "hh": ("sbuf", [128, 192], "bfloat16"), "sf": ("sbuf", [128, 192], "bfloat16"), "sb": ("sbuf", [128, 192], "bfloat16"),
+    "twin": ("sbuf", [128, 64], "float32"),
     "uu": ("sbuf", [128, 256], "float32"), "us": ("sbuf", [128, 256], "float32"), "off": ("sbuf", [128, 64], "uint16"),
 }
 for _n in ("px0", "px1", "px2", "px3", "px4", "px5", "pa", "pc"):
@@ -32,7 +33,7 @@ SEMAPHORES = (["sv", "sa", "sp", "sg", "sent", "stored", "lpk", "apk"]
 
 
 def col(v, swapped, who):
-    return Z + v * VB + swapped * 2048 + who * HB
+    return Z + v * VB + who * SL + swapped * HB
 
 
 def rank_program(g, core, T, topo):
@@ -133,7 +134,10 @@ def rank_program(g, core, T, topo):
     t_z = fill(W[:, 0:Z], 0.0)
     t_gh0 = fill(T.gh[:], 0.0)
     fill(T.lift[:], LIFT)
-    fill(T.uu[:], 8192.0 * STEP)
+    k = fill(T.uu[:], 0.0)
+    fill(T.twin[:, 0:32], float(mine[1]))
+    fill(T.twin[:, 32:64], float(mine[0]))
+    fill(T.uu[:, 0:256:4], 8192.0 * STEP, deps=[k])
     ts(T.ci[:, 2:3], T.ci[:, 1:2], 127, A.bitwise_and, deps=[t_ci])
     ts(T.ci[:, 3:4], T.ci[:, 0:1], 4, A.logical_shift_right, 3, A.bitwise_and)
     ts(T.ci[:, 4:5], T.ci[:, 0:1], 112, A.bitwise_and)
@@ -147,20 +151,19 @@ def rank_program(g, core, T, topo):
     ID, PM, M1, M2, M3, NS, LT, KI, K0 = [T.mats[:, i * 128:(i + 1) * 128] for i in range(9)]
     t_pm = ts(PM, T.mf[:, 0:128], px, A.is_equal, deps=[k, k_mf])
     ts(T.cf[:, 8:9], T.cf[:, 4:5], 15.0, A.add)
-    ts(T.cf[:, 9:10], ph, -2.0, A.mult, 1.0, A.add)
     ts(T.cf[:, 10:11], pf, 0.0, A.is_equal, SL * STEP, A.mult)
     ts(T.cf[:, 11:12], pf, 1.0, A.is_equal, 0.5 * STEP, A.mult)
     k_cf = ts(T.cf[:, 7:8], ph, 2048.0, A.mult)
-    p15, flip, sign = T.cf[:, 8:9], T.cf[:, 7:8], T.cf[:, 9:10]
+    p15, flip = T.cf[:, 8:9], T.cf[:, 7:8]
 
     def stationaries(R, pk, deps):
         for p in range(2):
             for i in range(2):
-                cp(T.gh[half(p), (2 * R + i) * 128 + 64 * p:(2 * R + i) * 128 + 64 * p + 64],
-                   pk[half(M), i * 128 + 64 * M:i * 128 + 64 * M + 64], deps=deps)
-            k2 = cp(T.wc[half(p), 8 * R:8 * R + 1], pk[half(M), 256:257])
+                kg = acp(T.gh[half(p), (2 * R + i) * 128 + 64 * p:(2 * R + i) * 128 + 64 * p + 64],
+                         pk[half(M), i * 128 + 64 * M:i * 128 + 64 * M + 64], deps=deps)
+            k2 = cp(T.wc[half(p), 8 * R:8 * R + 1], pk[half(M), 256:257], deps=deps)
         return ts(T.wb[:, R * 144:(R + 1) * 144], T.mf[:], p15, A.is_equal, T.wc[:, 8 * R:8 * R + 1], A.mult,
-                  deps=[k2, k_cf])
+                  deps=[k2, k_cf]), kg
 
     ts(ID, T.mf[:, 0:128], pf, A.is_equal)
     ts(M1, T.mj[:, 0:128], pg, A.is_equal, -STEP, A.mult, deps=[k_mj])
@@ -178,7 +181,7 @@ def rank_program(g, core, T, topo):
     k = tt(M3, LT, KI, A.add, deps=[k])
     fill(T.mats[64:128, 4 * 128:4 * 128 + 64], 0.0, deps=[k])
     cp(T.mats[0:64, 4 * 128 + 64:5 * 128], T.mats[0:64, 5 * 128 + 64:6 * 128])
-    t_w1 = stationaries(1, T.pk, [("lpk", 48), t_gh0])
+    t_w1, t_g1 = stationaries(1, T.pk, [("lpk", 48), t_gh0])
 
     every = topo.engines(core, cores[part])
     send([RemoteDMATransfer(dst_ids=[dst(part)], dma_engine_mask=bits(every), remote_sem=T.sem.apk,
@@ -224,17 +227,17 @@ def rank_program(g, core, T, topo):
         return mm([(T.pa[:, 32 * R:32 * R + 32], T.wb[:, R * 144 + 15 - q:R * 144 + 143 - q],
                     W[:, c + q:c + HB:16], q == 0, q == 15) for q in range(16)], deps=deps)
 
-    ai, who, hb, f1, jj = [T.xi[:, i * 64:(i + 1) * 64] for i in range(5)]
+    ai, who, av, f1, jj = [T.xi[:, i * 64:(i + 1) * 64] for i in range(5)]
 
     def chain_front(t, ka):
-        k = ts(ai, T.pa[:, 0:64], float(((S - t) % S) * VB), A.add, deps=[ka])
+        k = ts(ai, T.pa[:, 0:64], flip, A.add, deps=[ka])
+        k2 = ts(av, T.pa[:, 0:64], float(((S - t) % S) * VB), A.add)
         k = ts(who, ai, 3, A.bitwise_and, deps=[k])
-        ts(hb, ai, 2048, A.bitwise_and)
+        ts(jj, ai, 2, A.logical_shift_right, SL - 1, A.bitwise_and)
         ts(T.hh[:, 0:64], who, float(mate), A.is_equal, deps=[k])
         ts(T.hh[:, 64:128], who, float(pmate), A.is_equal)
-        ts(T.hh[:, 128:160], T.xi[:, 64:96], float(mine[1]), A.is_equal)
-        kh = ts(T.hh[:, 160:192], T.xi[:, 96:128], float(mine[0]), A.is_equal)
-        ts(jj, ai, 2, A.logical_shift_right, HB - 1, A.bitwise_and)
+        kh = tt(T.hh[:, 128:192], who, T.twin[:], A.is_equal)
+        ts(f1, av, 3 * VB, A.bitwise_and, deps=[k2])
         wait("v", [kh])
         kf = done("v", V.tensor_tensor_scan(T.sf[:], T.rst[:], T.hh[:], 0.0, A.mult, A.add))
         kb = done("v", V.tensor_tensor_scan(T.sb[:, ::-1], T.rst[:], T.hh[:, ::-1], 0.0, A.mult, A.add))
@@ -249,11 +252,9 @@ def rank_program(g, core, T, topo):
                      for i in range(3)], deps=[ko, ks[n]])
         return kc
 
-    def chain_back(t, kc):
-        k = ts(f1, ai, 3 * VB, A.bitwise_and)
-        ts(T.uu[:, 2:256:4], who, float(HB), A.mult)
-        ts(T.uu[:, 3:256:4], hb, sign, A.mult, flip, A.add)
-        k = tt(T.uu[:, 1:256:4], f1, jj, A.add, deps=[k])
+    def chain_back(t, ks, kc):
+        ts(T.uu[:, 2:256:4], who, float(SL), A.mult)
+        k = tt(T.uu[:, 1:256:4], f1, jj, A.add, deps=[ks[1]])
         wait("v", [k, kc])
         k = done("v", V.tensor_tensor_scan(T.us[:], T.uu[:], T.pc[:, 0:256], 0.0, A.add, A.min))
         return ts(T.off[:], T.us[:, 3:256:4], float(Z + t * VB), A.add, 0.0, A.max, deps=[k]), k
@@ -282,32 +283,37 @@ def rank_program(g, core, T, topo):
                          src[half(p), c:c + HB]).then_inc(T.sem.stored, 16)
             stores[0] += 16
 
+    turn = [0]
+
+    def swap_in(s, who):
+        turn[0] += 1
+        return swap_pe((4, 5, 1)[turn[0] % 3], s, who, [arrived(s, who)])
+
+    for s in order:
+        swap_in(s, r)
+    t_w0, t_g0 = stationaries(0, T.pkp, [("apk", len(topo.engines(cores[part], core)))])
     ko = open_count([t_w1])
-    for n, s in enumerate(order):
-        swap_pe(5 - n % 2, s, r, [arrived(s, r)])
-    t_w0 = stationaries(0, T.pkp, [("apk", len(topo.engines(cores[part], core)))])
     weigh(0, 1, [t_w1])
-    ahead(0, 2, "log")
-    ahead(0, 3, "log")
-    ka = weigh(0, 0, [t_w0, arrived(3, part)])
-    swap_pe(5, 3, part, [])
+    swap_in(3, part)
+    ka = weigh(0, 0, [t_w0])
     swap(cp, 3, mate, [arrived(3, mate)])
+    swap_in(3, pmate)
+    ahead(0, 2, "log", [t_g1])
     ks = chain_front(0, ka)
-    ahead(0, 0, "lg")
+    swap_in(0, mate)
     kc = count(ko, ks)
-    k_off, k_us = chain_back(0, kc)
-    swap(cp, 3, pmate, [arrived(3, pmate)])
-    ahead(0, 1, "lg")
-    for n, s in enumerate(order[1:]):
-        swap(cp, s, mate, [arrived(s, mate)])
-        k_sa = swap_pe(5 - n % 2, s, part, [arrived(s, part)])
-        if n < 2:
-            swap(cp, s, pmate, [arrived(s, pmate)])
-        else:
-            k_sv, k_sa = swap_both(s, pmate, [arrived(s, pmate)])
-        if n == 0:
-            ahead(0, 0, "o")
-            ahead(0, 1, "o")
+    k_off, k_us = chain_back(0, ks, kc)
+    swap_in(0, part)
+    ahead(0, 3, "log")
+    swap(cp, 0, pmate, [arrived(0, pmate)])
+    swap_in(1, mate)
+    ahead(0, 0, "log", [t_g0])
+    swap_in(1, part)
+    swap(cp, 1, pmate, [arrived(1, pmate)])
+    swap(cp, 2, mate, [arrived(2, mate)])
+    swap_pe(4, 2, part, [arrived(2, part)])
+    ahead(0, 1, "log")
+    k_sv, k_sa = swap_both(2, pmate, [arrived(2, pmate)], 256)
 
     near = topo.engines(core, cores[mate])
     far = topo.engines(core, cores[part])
@@ -387,7 +393,7 @@ def rank_program(g, core, T, topo):
         ahead(t + 1, 1, "g")
         ahead(t + 1, 2, "lo")
         kc = count(ko, ks)
-        k_off, k_us = chain_back(t + 1, kc)
+        k_off, k_us = chain_back(t + 1, ks, kc)
         k_sa = swap(acp, t + 4, theirs[0], [("wv%d_0" % t, n_in)])
         ahead(t + 1, 2, "g")
         ahead(t + 1, 3, "log")

@@ -1,35 +1,39 @@
 from concourse.bass import DstId, RemoteDMATransfer
 from concourse.mybir import AluOpType as A, ActivationFunctionType as F
 
-S, SL, HB, WAVES, CAP = 4, 1024, 512, 5, 320
+S, SL, HB, CH, WAVES, CAP = 4, 1024, 512, 256, 5, 320
 Z = 16
 VB = 4096
 KH = float(SL - CAP)
 STEP = 131072.0
 LIFT = 129.0 * 256.0
-OPT = {"last": "split", "gv": 896, "sendsw": 1, "x": 320}
+PK = 257
+RELAY = 3
+TWICE = (0, 1)
+OPT = {"gv": 896}
 
 SCRATCH = {
     "win": ("sbuf", [128, Z + 9 * VB], "bfloat16"), "oth": ("sbuf", [128, S * HB], "bfloat16"),
-    "back": ("sbuf", [128, S * HB], "bfloat16"), "pk": ("sbuf", [128, 272], "bfloat16"),
-    "pkp": ("sbuf", [128, 272], "bfloat16"), "gh": ("sbuf", [128, 512], "bfloat16"),
-    "wc": ("sbuf", [128, 16], "float32"), "wb": ("sbuf", [128, 288], "bfloat16"),
+    "back": ("sbuf", [128, S * HB], "bfloat16"), "pk": ("sbuf", [128, PK], "bfloat16"),
+    "pkp": ("sbuf", [128, PK], "bfloat16"), "gh": ("sbuf", [128, 512], "bfloat16"),
+    "wc": ("sbuf", [128, 24], "float32"), "wb": ("sbuf", [128, 3 * 144], "bfloat16"),
+    "offp": ("sbuf", [128, 32], "uint16"),
     "ref": ("sbuf", [128, SL], "bfloat16"), "rnd": ("sbuf", [128, SL], "bfloat16"),
-    "lift": ("sbuf", [128, 256], "bfloat16"), "mats": ("sbuf", [128, 9 * 128], "bfloat16"),
-    "ci": ("sbuf", [128, 8], "int32"), "cf": ("sbuf", [128, 16], "float32"), "mi": ("sbuf", [128, 256], "int32"),
-    "mj": ("sbuf", [128, 576], "int32"), "mf": ("sbuf", [128, 144], "float32"), "rst": ("sbuf", [128, 192], "bfloat16"),
-    "rs4": ("sbuf", [128, 256], "bfloat16"), "xi": ("sbuf", [128, 5 * 64], "int32"),
+    "lift": ("sbuf", [128, CH], "bfloat16"), "mats": ("sbuf", [128, 18 * 128], "bfloat16"),
+    "ci": ("sbuf", [128, 8], "int32"), "cf": ("sbuf", [128, 16], "float32"),
+    "mf": ("sbuf", [128, 144], "float32"), "key": ("sbuf", [128, 128], "float32"),
+    "rst": ("sbuf", [128, 192], "bfloat16"), "rs4": ("sbuf", [128, 256], "bfloat16"),
+    "xi": ("sbuf", [128, 5 * 64], "int32"),
     "hh": ("sbuf", [128, 192], "bfloat16"), "sf": ("sbuf", [128, 192], "bfloat16"), "sb": ("sbuf", [128, 192], "bfloat16"),
-    "twin": ("sbuf", [128, 64], "float32"),
     "uu": ("sbuf", [128, 256], "float32"), "us": ("sbuf", [128, 256], "float32"), "off": ("sbuf", [128, 64], "uint16"),
 }
 for _n in ("px0", "px1", "px2", "px3", "px4", "px5", "pa", "pc"):
     SCRATCH[_n] = ("psum", [128, 512], "float32")
-SEMAPHORES = (["sv", "sa", "sp", "sg", "sent", "stored", "lpk", "apk"]
+SEMAPHORES = (["sv", "sa", "sp", "sg", "sent", "stored", "lpk", "apk", "aoff", "soff", "lsw"]
               + ["lw%d" % s for s in range(S)] + ["lo%d" % s for s in range(S)]
               + ["in%d_%d" % (s, r) for s in range(S) for r in range(4)]
-              + ["wv%d_%d" % (t, b) for t in range(WAVES - 1) for b in range(3)]
-              + ["bk%d" % t for t in range(1, WAVES)])
+              + ["wv%d_%d" % (t, b) for t in range(WAVES - 1) for b in range(2)]
+              + ["bk%d" % t for t in range(1, WAVES + 1)])
 
 
 def col(v, swapped, who):
@@ -91,6 +95,10 @@ def rank_program(g, core, T, topo):
         wait("a", deps)
         return done("a", AC.activation(out, a, F.Copy))
 
+    def act(out, a, scale, bias, deps=()):
+        wait("a", deps)
+        return done("a", AC.activation(out, a, F.Identity, bias=bias, scale=scale))
+
     def fill(ap, c, deps=()):
         wait("v", deps)
         return done("v", V.memset(ap, c))
@@ -114,85 +122,97 @@ def rank_program(g, core, T, topo):
         return slice(64 * p, 64 * p + 64)
 
     order = [3, 0, 1, 2]
-    t_pad = fill(T.pk[:, 256:272], 0.0)
-    AC.dma_start(T.pk[:, 0:128], T.gm[:]).then_inc(T.sem.lpk, 16)
-    SY.dma_start(T.pk[:, 128:256], T.hm[:]).then_inc(T.sem.lpk, 16)
-    wait("a", [t_pad])
     AC.dma_start(T.pk[:, 256:257], T.kw[:]).then_inc(T.sem.lpk, 16)
+    SY.dma_start(T.pk[:, 128:256], T.hm[:]).then_inc(T.sem.lpk, 16)
+    AC.dma_start(T.pk[:, 0:128], T.gm[:]).then_inc(T.sem.lpk, 16)
     for n, s in enumerate(order):
-        dq = AC if n % 2 else SY
         c = col(s, 0, r)
         for p in range(2):
             src = slice(s * SL + p * HB, s * SL + (p + 1) * HB)
-            dq.dma_start(T.oth[half(p), s * HB:(s + 1) * HB], T.m[half(1 - M), src]).then_inc(T.sem["lo%d" % s], 16)
-        for p in range(2):
-            src = slice(s * SL + p * HB, s * SL + (p + 1) * HB)
-            dq.dma_start(W[half(p), c:c + HB], T.m[half(M), src]).then_inc(T.sem["lw%d" % s], 16)
+            SY.dma_start(T.oth[half(p), s * HB:(s + 1) * HB], T.m[half(1 - M), src]).then_inc(T.sem["lo%d" % s], 16)
+            AC.dma_start(W[half(p), c:c + HB], T.m[half(M), src]).then_inc(T.sem["lw%d" % s], 16)
+
+    for s in order[1:]:
+        c = col(s, 1, r)
+        for p, dq in enumerate((SY, AC)):
+            src = slice(s * SL + (1 - p) * HB, s * SL + (2 - p) * HB)
+            dq.dma_start(W[half(p), c:c + HB], T.m[half(M), src]).then_inc(T.sem.lsw, 16)
 
     t_ci = done("g", g.iota(T.ci[:, 0:2], [[64, 2]], 0, 1))
-    t_mi = done("g", g.iota(T.mi[:], [[1, 256]], 0, 0))
-    t_z = fill(W[:, 0:Z], 0.0)
+    t_mf = done("g", g.iota(T.mf[:], [[1, 144]], 0, 0, allow_small_or_imprecise_dtypes=True))
+    t_key = done("g", g.iota(T.key[:], [[16, 2], [32, 4], [1, 16]], 0, 0, allow_small_or_imprecise_dtypes=True))
+    ID, PM, M1, M2, M3, S1, S2, S3, S4, NI, KI, K0 = [T.mats[:, i * 128:(i + 1) * 128] for i in range(12)]
     t_gh0 = fill(T.gh[:], 0.0)
-    fill(T.lift[:], LIFT)
-    k = fill(T.uu[:], 0.0)
-    fill(T.twin[:, 0:32], float(mine[1]))
-    fill(T.twin[:, 32:64], float(mine[0]))
-    fill(T.uu[:, 0:256:4], 8192.0 * STEP, deps=[k])
-    ts(T.ci[:, 2:3], T.ci[:, 1:2], 127, A.bitwise_and, deps=[t_ci])
-    ts(T.ci[:, 3:4], T.ci[:, 0:1], 4, A.logical_shift_right, 3, A.bitwise_and)
-    ts(T.ci[:, 4:5], T.ci[:, 0:1], 112, A.bitwise_and)
-    k = ts(T.ci[:, 5:6], T.ci[:, 0:1], 6, A.logical_shift_right)
-    k_mf = cp(T.mf[:], T.mi[:, 0:144], deps=[t_mi])
-    ts(T.mj[:, 0:128], T.mi[:, 0:128], 4, A.logical_shift_right, 3, A.bitwise_and)
-    ts(T.mj[:, 320:576], T.mi[:], 3, A.bitwise_and)
-    k_mj = ts(T.mj[:, 128:320], T.mi[:, 0:192], 31, A.bitwise_and)
-    k = cp(T.cf[:, 0:6], T.ci[:, 0:6], deps=[k])
-    pf, px, pg, ph = T.cf[:, 0:1], T.cf[:, 2:3], T.cf[:, 3:4], T.cf[:, 5:6]
-    ID, PM, M1, M2, M3, NS, LT, KI, K0 = [T.mats[:, i * 128:(i + 1) * 128] for i in range(9)]
-    t_pm = ts(PM, T.mf[:, 0:128], px, A.is_equal, deps=[k, k_mf])
-    ts(T.cf[:, 8:9], T.cf[:, 4:5], 15.0, A.add)
-    ts(T.cf[:, 10:11], pf, 0.0, A.is_equal, SL * STEP, A.mult)
-    ts(T.cf[:, 11:12], pf, 1.0, A.is_equal, 0.5 * STEP, A.mult)
-    k_cf = ts(T.cf[:, 7:8], ph, 2048.0, A.mult)
-    p15, flip = T.cf[:, 8:9], T.cf[:, 7:8]
+    act(T.rs4[0:64, :], T.gh[0:64, 0:256], 1.0, 1.0, deps=[t_gh0])
+    act(T.rst[:], T.gh[:, 0:192], 1.0, 1.0)
+    k1 = act(T.uu[:], T.gh[:, 0:256], 1.0, 0.0)
+    act(T.lift[:], T.gh[:, 0:CH], 1.0, LIFT)
+    for i, (sh, mask) in enumerate(((4, 3), (0, 112), (6, 1), (0, 15))):
+        ts(T.ci[:, 3 + i:4 + i], T.ci[:, 0:1], sh, A.logical_shift_right, mask, A.bitwise_and, deps=[t_ci])
+    k = ts(T.ci[:, 2:3], T.ci[:, 1:2], 127, A.bitwise_and)
+    k4 = fill(T.rs4[64:96, :], 0.0)
+    k = cp(T.cf[:, 0:7], T.ci[:, 0:7], deps=[k])
+    t_z = fill(W[:, 0:Z], 0.0)
+    pf, px, pg, p0, ph, pq = [T.cf[:, i:i + 1] for i in (0, 2, 3, 4, 5, 6)]
+    p15, flip, low, seg = [T.cf[:, i:i + 1] for i in range(8, 12)]
+    k = ts(low, pg, 32.0, A.mult, deps=[k])
+    ts(p15, p0, 15.0, A.add)
+    t_id = ts(ID, T.mf[:, 0:128], pf, A.is_equal, deps=[t_mf])
+    t_pm = ts(PM, T.mf[:, 0:128], px, A.is_equal)
+    k_cf = ts(seg, ph, 16.0, A.mult, low, A.add, deps=[k])
+    ts(flip, ph, 2048.0, A.mult)
 
-    def stationaries(R, pk, deps):
+    def matrices(R, pk, deps):
         for p in range(2):
             for i in range(2):
                 kg = acp(T.gh[half(p), (2 * R + i) * 128 + 64 * p:(2 * R + i) * 128 + 64 * p + 64],
                          pk[half(M), i * 128 + 64 * M:i * 128 + 64 * M + 64], deps=deps)
-            k2 = cp(T.wc[half(p), 8 * R:8 * R + 1], pk[half(M), 256:257], deps=deps)
-        return ts(T.wb[:, R * 144:(R + 1) * 144], T.mf[:], p15, A.is_equal, T.wc[:, 8 * R:8 * R + 1], A.mult,
-                  deps=[k2, k_cf]), kg
+        return kg
 
-    ts(ID, T.mf[:, 0:128], pf, A.is_equal)
-    ts(M1, T.mj[:, 0:128], pg, A.is_equal, -STEP, A.mult, deps=[k_mj])
-    ts(NS, T.mj[:, 0:128], pg, A.is_equal, STEP, A.mult)
-    ts(LT, T.mf[:, 0:128], pf, A.is_lt)
-    ts(KI, T.mf[:, 0:128], pf, A.is_equal, -KH * STEP, A.mult)
-    k0 = tt(T.cf[:, 12:13], T.cf[:, 10:11], T.cf[:, 11:12], A.add, deps=[k_cf])
-    fill(M2, 0.0)
-    ts(T.rs4[:], T.mj[:, 320:576], 0.0, A.is_gt)
-    k = ts(T.rst[:], T.mj[:, 128:320], 0.0, A.is_gt)
-    ts(K0, T.mf[:, 0:128], -1.0, A.is_gt, T.cf[:, 12:13], A.mult, deps=[k0])
-    k = tt(LT, LT, NS, A.mult, deps=[k])
-    cp(T.mats[0:64, 3 * 128 + 64:4 * 128], T.mats[0:64, 2 * 128 + 64:3 * 128])
-    fill(T.mats[64:128, 2 * 128:2 * 128 + 64], 0.0)
-    k = tt(M3, LT, KI, A.add, deps=[k])
-    fill(T.mats[64:128, 4 * 128:4 * 128 + 64], 0.0, deps=[k])
-    cp(T.mats[0:64, 4 * 128 + 64:5 * 128], T.mats[0:64, 5 * 128 + 64:6 * 128])
-    t_w1, t_g1 = stationaries(1, T.pk, [("lpk", 48), t_gh0])
+    def weights(jobs, deps):
+        for n, pk, rows in jobs:
+            for p in range(2):
+                k = cp(T.wc[half(p), 8 * n:8 * n + 1], pk[half(rows), 256:257], deps=deps)
+        for n, pk, rows in jobs:
+            k2 = ts(T.wb[:, n * 144:(n + 1) * 144], T.mf[:], p15, A.is_equal, T.wc[:, 8 * n:8 * n + 1], A.mult, deps=[k])
+        return k2
 
-    every = topo.engines(core, cores[part])
+    t_w1 = weights([(2, T.pk, 1 - M), (1, T.pk, M)], [("lpk", 48), k_cf])
+    ts(S1, T.key[:], seg, A.subtract, 16.0, A.is_ge, deps=[t_key])
+    ts(S2, T.key[:], seg, A.is_ge)
+    ts(S3, T.key[:], low, A.subtract, 32.0, A.is_ge)
+    t_s = ts(S4, T.key[:], seg, A.subtract, pq, A.is_ge)
+    fill(T.rs4[0:64, 0:256:4], 0.0, deps=[k1])
+    fill(T.rst[:, 0:192:32], 0.0)
+    fill(T.uu[:, 0:256:4], 8192.0 * STEP)
+    fill(T.mats[0:32, 11 * 128:12 * 128], SL / 32 * STEP)
+    fill(T.mats[32:64, 11 * 128:12 * 128], STEP / 64)
+    fill(T.mats[64:96, 11 * 128:12 * 128], SL / 32)
+    t_k0 = fill(T.rs4[64:96, 0:256:4], float(r), deps=[k4])
+    t_g1 = matrices(1, T.pk, [("lpk", 48)])
+    act(NI, ID, -1.0, 0.0, deps=[t_id])
+    k = act(KI, ID, -KH, 0.0)
+    others = [[mate, pmate, mine[1 - R]] for R in range(2)]
+    hops = sorted(set(q - mine[R] for R in range(2) for q in others[R]))
+    hop = {d: T.mats[:, (12 + n) * 128:(13 + n) * 128] for n, d in enumerate(hops)}
+    for d in hops:
+        act(hop[d], ID, float(d * SL), 0.0)
+    items = []
+    for i, terms in enumerate((((ID, S3), (NI, S2)), ((ID, S3), (NI, S1)),
+                               ((ID, S1), (ID, S2), (NI, S4), (NI, S3), (KI, ID)))):
+        items += [(T.px0[:, 128 * i:128 * i + 128], a, b, n == 0, n == len(terms) - 1) for n, (a, b) in enumerate(terms)]
+
+    every = topo.engines(core, cores[part])[1::2]
     send([RemoteDMATransfer(dst_ids=[dst(part)], dma_engine_mask=bits(every), remote_sem=T.sem.apk,
                             src=T.pk[:], dst=T.pkp[:])], len(every), [("lpk", 48)])
+    far = topo.engines(core, cores[part])[0::2]
+    near = topo.engines(core, cores[mate])[1::2]
     for n, s in enumerate(order):
-        far = topo.engines(core, cores[part])[n % 2::2]
-        near = topo.engines(core, cores[mate])[1 - n % 2::2]
         c = col(s, 0, r)
         sem = T.sem["in%d_%d" % (s, r)]
-        send([RemoteDMATransfer(dst_ids=[dst(part), dst(pmate)], dma_engine_mask=bits(far), remote_sem=sem,
-                                src=T.oth[:, s * HB:(s + 1) * HB], dsts=[W[:, c:c + HB], W[:, c:c + HB]]),
+        to = [part] if n < RELAY else [part, pmate]
+        send([RemoteDMATransfer(dst_ids=[dst(q) for q in to], dma_engine_mask=bits(far), remote_sem=sem,
+                                src=T.oth[:, s * HB:(s + 1) * HB], dsts=[W[:, c:c + HB] for q in to]),
               RemoteDMATransfer(dst_ids=[dst(mate)], dma_engine_mask=bits(near), remote_sem=sem,
                                 src=W[:, c:c + HB], dst=W[:, c:c + HB])],
              len(far) + len(near), [("lo%d" % s, 32), ("lw%d" % s, 32)])
@@ -204,11 +224,11 @@ def rank_program(g, core, T, topo):
 
     freed = {}
 
-    def swap_pe(b, v, who, deps):
-        ps = T["px%d" % b]
-        c, d = col(v, 0, who), col(v, 1, who)
-        kp = mm([(ps[:], PM, W[:, c:c + HB], True, True)], deps=list(deps) + [freed.get(b), t_pm])
-        freed[b] = acp(W[:, d:d + HB], ps[:], deps=[kp])
+    def swap_pe(b, v, who, deps, o=0, n=HB):
+        ps = T["px%d" % b][:, 0:n]
+        c, d = col(v, 0, who) + o, col(v, 1, who) + o
+        kp = mm([(ps, PM, W[:, c:c + n], True, True)], deps=list(deps) + [freed.get(b), t_pm])
+        freed[b] = acp(W[:, d:d + n], ps, deps=[kp])
         return freed[b]
 
     def swap(op, v, who, deps, o=0, n=HB):
@@ -216,16 +236,16 @@ def rank_program(g, core, T, topo):
         op(W[half(0), d:d + n], W[half(1), c:c + n], deps=deps)
         return op(W[half(1), d:d + n], W[half(0), c:c + n])
 
-    def swap_both(v, who, deps, x=160):
+    def swap_both(v, who, deps, x):
         c, d = col(v, 0, who), col(v, 1, who)
         ka = acp(W[half(1), d + x:d + HB], W[half(0), c + x:c + HB], deps=deps)
         cp(W[half(0), d:d + HB], W[half(1), c:c + HB], deps=deps)
         return cp(W[half(1), d:d + x], W[half(0), c:c + x]), ka
 
     def weigh(t, R, deps):
-        c = col(t + 3, 0, mine[R])
-        return mm([(T.pa[:, 32 * R:32 * R + 32], T.wb[:, R * 144 + 15 - q:R * 144 + 143 - q],
-                    W[:, c + q:c + HB:16], q == 0, q == 15) for q in range(16)], deps=deps)
+        n, src, c = (2, T.oth, 3 * HB) if t == R == 0 else (R, W, col(t + 3, 0, mine[R]))
+        return mm([(T.pa[:, 32 * R:32 * R + 32], T.wb[:, n * 144 + 15 - q:n * 144 + 143 - q],
+                    src[:, c + q:c + HB:16], q == 0, q == 15) for q in range(16)], deps=deps)
 
     ai, who, av, f1, jj = [T.xi[:, i * 64:(i + 1) * 64] for i in range(5)]
 
@@ -234,86 +254,109 @@ def rank_program(g, core, T, topo):
         k2 = ts(av, T.pa[:, 0:64], float(((S - t) % S) * VB), A.add)
         k = ts(who, ai, 3, A.bitwise_and, deps=[k])
         ts(jj, ai, 2, A.logical_shift_right, SL - 1, A.bitwise_and)
-        ts(T.hh[:, 0:64], who, float(mate), A.is_equal, deps=[k])
-        ts(T.hh[:, 64:128], who, float(pmate), A.is_equal)
-        kh = tt(T.hh[:, 128:192], who, T.twin[:], A.is_equal)
+        kh = [ts(T.hh[:, 0:64], who, float(mate), A.is_equal, deps=[k]),
+              ts(T.hh[:, 64:128], who, float(pmate), A.is_equal),
+              tt(T.hh[:, 128:192], who, T.pa[:, 64:128], A.is_equal) if t else
+              ts(T.hh[:, 128:192], who, float(part), A.is_equal)]
         ts(f1, av, 3 * VB, A.bitwise_and, deps=[k2])
-        wait("v", [kh])
+        wait("v", kh)
         kf = done("v", V.tensor_tensor_scan(T.sf[:], T.rst[:], T.hh[:], 0.0, A.mult, A.add))
         kb = done("v", V.tensor_tensor_scan(T.sb[:, ::-1], T.rst[:], T.hh[:, ::-1], 0.0, A.mult, A.add))
         return kh, kf, kb
 
     def open_count(deps):
-        return mm([(T.pc[:, 0:256], K0, T.rs4[:], True, False)], deps=deps)
+        return mm([(T.pc[:, 0:256], T.mats[0:96, 11 * 128:12 * 128], T.rs4[0:96, :], True, False)], deps=deps)
 
-    def count(ko, ks):
-        for n, (mat, src) in enumerate(((M3, T.hh), (M1, T.sf), (M2, T.sb))):
-            kc = mm([(T.pc[:, 1 + i:256:4], mat, src[:, 64 * i:64 * i + 64], False, n == 2 and i == 2)
-                     for i in range(3)], deps=[ko, ks[n]])
+    def count(t, ko, ks):
+        for i in range(3):
+            mm([(T.pc[:, 128 * R:128 * R + 128:4], hop[others[own][i] - mine[own]],
+                 T.hh[:, 64 * i + 32 * R:64 * i + 32 * R + 32], False, False)
+                for R, own in enumerate((0, 1) if t else (1, 1))]
+               + [(T.pc[:, 1 + i:256:4], M3, T.hh[:, 64 * i:64 * i + 64], False, False)], deps=[ko, ks[0][i], t_m])
+        for n, (mat, src) in enumerate(((M1, T.sf), (M2, T.sb))):
+            kc = mm([(T.pc[:, 1 + i:256:4], mat, src[:, 64 * i:64 * i + 64], False, n == 1 and i == 2)
+                     for i in range(3)], deps=[ks[n + 1]])
         return kc
 
     def chain_back(t, ks, kc):
-        ts(T.uu[:, 2:256:4], who, float(SL), A.mult)
         k = tt(T.uu[:, 1:256:4], f1, jj, A.add, deps=[ks[1]])
         wait("v", [k, kc])
         k = done("v", V.tensor_tensor_scan(T.us[:], T.uu[:], T.pc[:, 0:256], 0.0, A.add, A.min))
         return ts(T.off[:], T.us[:, 3:256:4], float(Z + t * VB), A.add, 0.0, A.max, deps=[k]), k
 
+    def bank(t, kk):
+        return (4 * t + kk) % 6
+
+    def chunk(t, kk):
+        if t < WAVES - 1 or kk in (2, 3):
+            return kk // 2, (kk % 2) * CH, CH
+        return 0, (kk % 2 + kk // 2) * CH // 2, CH // 2
+
     def acc(t, kk):
-        return T["px%d" % ((4 * t + kk) % 6)][:, 0:256]
+        return T["px%d" % bank(t, kk)][:, 0:chunk(t, kk)[2]]
 
     def ahead(t, kk, what, deps=()):
-        R, o = kk // 2, (kk % 2) * 256
+        R, o, n = chunk(t, kk)
         cprev, cold = col(t + 3, 0, mine[R]) + o, col(t, 0, mine[R]) + o
-        wait("p", list(deps) + [freed.get((4 * t + kk) % 6)])
+        wait("p", list(deps) + [freed.get(bank(t, kk))])
         if "l" in what:
-            PE.matmul(acc(t, kk), ID, T.lift[:], True, False)
+            PE.matmul(acc(t, kk), ID, T.lift[:, 0:n], True, False)
         if "o" in what:
-            PE.matmul(acc(t, kk), ID, W[:, cold:cold + 256], False, False)
+            PE.matmul(acc(t, kk), ID, W[:, cold:cold + n], False, False)
         if "g" in what:
-            PE.matmul(acc(t, kk), T.gh[:, 2 * R * 128:(2 * R + 1) * 128], W[:, cprev:cprev + 256], False, False)
+            PE.matmul(acc(t, kk), T.gh[:, 2 * R * 128:(2 * R + 1) * 128], W[:, cprev:cprev + n], False, False)
 
     stores = [0]
 
-    def store(t, src, c, rows, deps):
-        s = t % S
-        wait("s", deps)
+    def store(t, src, c, rows, deps, o=0, n=HB, qn="s"):
+        y = (t % S) * SL + o
+        wait(qn, deps)
         for p in range(2):
-            SY.dma_start(T.y[half(rows), s * SL + p * HB:s * SL + (p + 1) * HB],
-                         src[half(p), c:c + HB]).then_inc(T.sem.stored, 16)
+            Q[qn][0].dma_start(T.y[half(rows), y + p * HB:y + p * HB + n],
+                               src[half(p), c + o:c + o + n]).then_inc(T.sem.stored, 16)
             stores[0] += 16
 
-    turn = [0]
+    def hand_on(s, swapped, es, deps):
+        c = col(s, swapped, part)
+        send([RemoteDMATransfer(dst_ids=[dst(mate)], dma_engine_mask=bits(es), remote_sem=T.sem["in%d_%d" % (s, part)],
+                                src=W[:, c:c + HB], dst=W[:, c:c + HB])], len(es), deps)
 
-    def swap_in(s, who):
-        turn[0] += 1
-        return swap_pe((4, 5, 1)[turn[0] % 3], s, who, [arrived(s, who)])
-
-    for s in order:
-        swap_in(s, r)
-    t_w0, t_g0 = stationaries(0, T.pkp, [("apk", len(topo.engines(cores[part], core)))])
-    ko = open_count([t_w1])
-    weigh(0, 1, [t_w1])
-    swap_in(3, part)
-    ka = weigh(0, 0, [t_w0])
-    swap(cp, 3, mate, [arrived(3, mate)])
-    swap_in(3, pmate)
-    ahead(0, 2, "log", [t_g1])
+    both = topo.engines(core, cores[mate])
+    weigh(0, 0, [t_w1, ("lo3", 32)])
+    ka = weigh(0, 1, [arrived(3, r)])
+    k = mm(items, deps=[k, t_s])
+    swap(acp, 3, r, [arrived(3, r)])
+    t_m = freed[0] = act(T.mats[:, 256:640], T.px0[:, 0:384], STEP, 0.0, deps=[k])
+    ko = open_count([t_k0])
+    swap_pe(5, 3, part, [arrived(3, part)])
     ks = chain_front(0, ka)
-    swap_in(0, mate)
-    kc = count(ko, ks)
+    kc = count(0, ko, ks)
+    swap(cp, 3, mate, [arrived(3, mate)])
     k_off, k_us = chain_back(0, ks, kc)
-    swap_in(0, part)
-    ahead(0, 3, "log")
-    swap(cp, 0, pmate, [arrived(0, pmate)])
-    swap_in(1, mate)
-    ahead(0, 0, "log", [t_g0])
-    swap_in(1, part)
-    swap(cp, 1, pmate, [arrived(1, pmate)])
-    swap(cp, 2, mate, [arrived(2, mate)])
-    swap_pe(4, 2, part, [arrived(2, part)])
-    ahead(0, 1, "log")
-    k_sv, k_sa = swap_both(2, pmate, [arrived(2, pmate)], 256)
+    turned = {s: swap_pe(b, s, part, [arrived(s, part)]) for s, b in ((0, 1), (1, 4), (2, 5))}
+    for s in order[:RELAY]:
+        hand_on(s, 0, near, [arrived(s, part)])
+    wait("g", [k_off])
+    g.remote_dma_fused([RemoteDMATransfer(dst_ids=[dst(part)], dma_engine_mask=bits(far), remote_sem=T.sem.aoff,
+                                          src=T.off[:, 0:32], dst=T.offp[:])], local_sem=T.sem.soff)
+    k_aoff = ("soff", len(every))
+    for s in TWICE:
+        hand_on(s, 1, both, [turned[s]])
+    t_g0 = matrices(0, T.pkp, [("apk", len(every))])
+    act(T.pa[:, 64:96], T.lift[:, 0:32], 0.0, float(mine[1]), deps=[k_off])
+    act(T.pa[:, 96:128], T.lift[:, 0:32], 0.0, float(mine[0]))
+    act(T.rs4[64:96, 0:128:4], T.lift[64:96, 0:32], 0.0, float(part), deps=[ko])
+    for p in range(2):
+        k = acp(T.wc[half(p), 0:1], T.pkp[half(M), 256:257])
+    for kk in (2, 3, 0, 1):
+        ahead(0, kk, "log", [arrived(0, r), t_g1] + ([t_g0] if kk < 2 else []))
+    for s, q in ((0, mate), (1, mate), (2, mate), (3, pmate)):
+        swap(cp, s, q, [arrived(s, q)])
+    k_sv, k_sa = swap_both(2, pmate, [arrived(2, pmate)], 192)
+    t_w0 = ts(T.wb[:, 0:144], T.mf[:], p15, A.is_equal, T.wc[:, 0:1], A.mult, deps=[k])
+    for qn in "va":
+        wait(qn, [arrived(s, r) for s in order] + [("lsw", 96)]
+             + [("in%d_%d" % (s, pmate), len(near) + len(both)) for s in TWICE])
 
     near = topo.engines(core, cores[mate])
     far = topo.engines(core, cores[part])
@@ -324,85 +367,84 @@ def rank_program(g, core, T, topo):
         ready = [k_off, k_sv, k_sa, t_z]
         last = t == WAVES - 1
 
-        def gv(a, b):
-            return cp(T.ref[:, a:b], win.indirect(T.off[:, a // 16:b // 16]), deps=ready)
-
-        def ga(a, b):
-            return acp(T.ref[:, a:b], win.indirect(T.off[:, a // 16:b // 16]), deps=ready)
+        def gather(op, a, b):
+            if t == 0 and a < HB:
+                return op(T.ref[:, a:b], win.indirect(T.offp[:, a // 16:b // 16]), deps=ready + [("aoff", len(every))])
+            return op(T.ref[:, a:b], win.indirect(T.off[:, a // 16:b // 16]), deps=ready)
 
         def finish(kk, deps):
-            R, o = kk // 2, (kk % 2) * 256
+            R, o, n = chunk(t, kk)
             px_ = acc(t, kk)
-            cs = slice(kk * 256, (kk + 1) * 256)
+            cs = slice(R * HB + o, R * HB + o + n)
             kh = mm([(px_, T.gh[:, (2 * R + 1) * 128:(2 * R + 2) * 128], T.ref[:, cs], False, True)], deps=deps)
-            wait("a", [kh])
-            kr = done("a", AC.activation(T.rnd[:, cs], px_, F.Identity, bias=-127.5))
+            kr = act(T.rnd[:, cs], px_, 1.0, -127.5, deps=[kh])
             c = col(t + 4, 0, mine[R]) + o
-            freed[(4 * t + kk) % 6] = tt(W[:, c:c + 256], px_, T.rnd[:, cs], A.subtract, deps=[kr])
-            return freed[(4 * t + kk) % 6]
+            freed[bank(t, kk)] = tt(W[:, c:c + n], px_, T.rnd[:, cs], A.subtract, deps=[kr])
+            return freed[bank(t, kk)]
 
         if 2 <= t:
             store(t - 1, W, col(t + 3, 0, r), M, [k_off])
-            if last:
-                store(t - 1, T.back, ((t - 1) % S) * HB, 1 - M, [("bk%d" % (t - 1), n_back)])
         c0, c1 = col(t + 4, 0, mine[0]), col(t + 4, 0, mine[1])
 
-        def back(deps):
-            o = (t % S) * HB
-            send([RemoteDMATransfer(dst_ids=[dst(part)], dma_engine_mask=bits(far), remote_sem=T.sem["bk%d" % t],
-                                    src=W[:, c0:c0 + HB], dst=T.back[:, o:o + HB])], len(far), deps)
+        def back(deps, i=0, n=HB):
+            o = (t % S) * HB + i * n
+            send([RemoteDMATransfer(dst_ids=[dst(part)], dma_engine_mask=bits(far), remote_sem=T.sem["bk%d" % (t + i)],
+                                    src=W[:, c0 + i * n:c0 + i * n + n], dst=T.back[:, o:o + n])], len(far), deps)
 
+        def store_back(t, deps):
+            store(t, T.back, (t % S) * HB, 1 - M, [("bk%d" % t, n_back)] + deps)
+
+        if 2 <= t:
+            store_back(t - 1, [])
         if last:
-            g0 = gv(0, 256)
-            g1 = ga(256, 512)
-            g3 = gv(512, 768)
-            finish(0, [g0])
-            n1 = finish(1, [g1])
-            back([n1])
-            g4 = ga(768, 1024)
-            finish(2, [g3])
-            n3 = finish(3, [g4])
-            store(t, W, c1, M, [n3])
-            store(t, T.back, (t % S) * HB, 1 - M, [("bk%d" % t, n_back)])
+            ga = [gather(cp, 0, 128), gather(acp, 128, 256), gather(cp, 256, 384), gather(acp, 384, 512)]
+            g2 = gather(cp, 512, 640)
+            for n, kk in enumerate((0, 1, 4, 5)):
+                k = finish(kk, ga[n:n + 1])
+                if n % 2:
+                    back([k], n // 2, CH)
+            ahead(t, 2, "g")
+            ahead(t, 3, "log")
+            g3 = gather(acp, 640, 768)
+            g4 = gather(cp, 768, 1024)
+            new = [finish(2, [g2, g3]), finish(3, [g4])]
+            for i in range(2):
+                store(t, W, c1, M, [new[i]], i * CH, CH)
+                store(t, T.back, 0, 1 - M, [("bk%d" % (t + i), n_back)], i * CH, CH, "a")
             break
         x = OPT["gv"]
-        g0 = gv(0, 256)
-        g1 = ga(256, 512)
-        g2 = gv(512, 768)
-        g3 = gv(768, x)
-        g4 = ga(x, 1024)
-        ko = open_count([k_us])
+        ga = [gather(cp, 0, 256), gather(acp, 256, 512)]
+        gb = [gather(cp, 512, 768), gather(cp, 768, x), gather(acp, x, 1024)]
+        ko = open_count([k_us, t_w0])
         ahead(t + 1, 0, "lo")
-        new = [finish(0, [g0]), finish(1, [g1])]
+        new = [finish(0, ga[:1]), finish(1, ga[1:])]
         ahead(t + 1, 1, "lo")
-        new += [finish(2, [g2]), finish(3, [g3, g4])]
-        k_own = swap(cp, t + 4, mine[1], [new[3]])
-        for b, (c, kk) in enumerate(((c0, new[1]), (c1, new[3]), (col(t + 4, 1, mine[1]), k_own))[:2 + OPT["sendsw"]]):
-            send([RemoteDMATransfer(dst_ids=[dst(mate)], dma_engine_mask=bits(near), remote_sem=T.sem["wv%d_%d" % (t, min(b, 1))],
-                                    src=W[:, c:c + HB], dst=W[:, c:c + HB])], len(near), [kk])
+        new += [finish(2, gb[:1]), finish(3, gb[1:])]
+        k_own = [swap(acp, t + 4, mine[1], [new[2]], 0, CH), swap(cp, t + 4, mine[1], [new[3]], CH, CH)]
+        for b, (c, deps) in enumerate(((c0, [new[1]]), (c1, [new[3]]), (col(t + 4, 1, mine[1]), k_own))):
+            send([RemoteDMATransfer(dst_ids=[dst(mate)], dma_engine_mask=bits(near),
+                                    remote_sem=T.sem["wv%d_%d" % (t, min(b, 1))],
+                                    src=W[:, c:c + HB], dst=W[:, c:c + HB])], len(near), deps)
+        if t >= 1:
+            back([])
         weigh(t + 1, 0, [new[1]])
         ka = weigh(t + 1, 1, [new[3]])
-        left = ("sent", sent[0])
-        if t >= 2:
-            store(t - 1, T.back, ((t - 1) % S) * HB, 1 - M, [("bk%d" % (t - 1), n_back), left])
-        if t >= 1:
-            back([left])
         swap(acp, t + 4, mine[0], [new[1]])
         ks = chain_front(t + 1, ka)
         ahead(t + 1, 0, "g")
         ahead(t + 1, 1, "g")
         ahead(t + 1, 2, "lo")
-        kc = count(ko, ks)
+        kc = count(t + 1, ko, ks)
+        wait("v", [k_aoff])
         k_off, k_us = chain_back(t + 1, ks, kc)
         k_sa = swap(acp, t + 4, theirs[0], [("wv%d_0" % t, n_in)])
-        ahead(t + 1, 2, "g")
-        ahead(t + 1, 3, "log")
-        if OPT["sendsw"]:
-            k_sv = ("wv%d_1" % t, 2 * n_in)
-        elif OPT["last"] == "split":
-            k_sv, k_sa = swap_both(t + 4, theirs[1], [("wv%d_1" % t, n_in)], OPT["x"])
+        if t + 2 == WAVES:
+            ahead(t + 1, 4, "log")
+            ahead(t + 1, 5, "log")
         else:
-            k_sa = swap_pe((4 * t + 2) % 6, t + 4, theirs[1], [("wv%d_1" % t, n_in)])
+            ahead(t + 1, 2, "g")
+            ahead(t + 1, 3, "log")
+        k_sv = ("wv%d_1" % t, 2 * n_in)
 
     wait("s", [("stored", stores[0])])
     wait("g", [("sent", sent[0]), ("sv", Q["v"][2]), ("sa", Q["a"][2]), ("sp", Q["p"][2]), ("sg", Q["g"][2])])

from concourse.bass import DstId, RemoteDMATransfer
from concourse.mybir import AluOpType as A, ActivationFunctionType as F

S, SL, HB, CH, WAVES, CAP = 4, 1024, 512, 256, 5, 320
Z = 16
VB = 4096
KH = float(SL - CAP)
STEP = 131072.0
LIFT = 129.0 * 256.0
PK = 257
RELAY = 3
TWICE = (0, 1)
OPT = {"gv": 896}

SCRATCH = {
    "win": ("sbuf", [128, Z + 9 * VB], "bfloat16"), "oth": ("sbuf", [128, S * HB], "bfloat16"),
    "back": ("sbuf", [128, S * HB], "bfloat16"), "pk": ("sbuf", [128, PK], "bfloat16"),
    "pkp": ("sbuf", [128, PK], "bfloat16"), "gh": ("sbuf", [128, 512], "bfloat16"),
    "wc": ("sbuf", [128, 24], "float32"), "wb": ("sbuf", [128, 3 * 144], "bfloat16"),
    "offp": ("sbuf", [128, 32], "uint16"),
    "ref": ("sbuf", [128, SL], "bfloat16"), "rnd": ("sbuf", [128, SL], "bfloat16"),
    "lift": ("sbuf", [128, CH], "bfloat16"), "mats": ("sbuf", [128, 18 * 128], "bfloat16"),
    "ci": ("sbuf", [128, 8], "int32"), "cf": ("sbuf", [128, 16], "float32"),
    "mf": ("sbuf", [128, 144], "float32"), "key": ("sbuf", [128, 128], "float32"),
    "rst": ("sbuf", [128, 192], "bfloat16"), "rs4": ("sbuf", [128, 256], "bfloat16"),
    "xi": ("sbuf", [128, 5 * 64], "int32"),
    "hh": ("sbuf", [128, 192], "bfloat16"), "sf": ("sbuf", [128, 192], "bfloat16"), "sb": ("sbuf", [128, 192], "bfloat16"),
    "uu": ("sbuf", [128, 256], "float32"), "us": ("sbuf", [128, 256], "float32"), "off": ("sbuf", [128, 64], "uint16"),
}
for _n in ("px0", "px1", "px2", "px3", "px4", "px5", "pa", "pc"):
    SCRATCH[_n] = ("psum", [128, 512], "float32")
SEMAPHORES = (["sv", "sa", "sp", "sg", "sent", "stored", "lpk", "apk", "aoff", "soff", "lsw"]
              + ["lw%d" % s for s in range(S)] + ["lo%d" % s for s in range(S)]
              + ["in%d_%d" % (s, r) for s in range(S) for r in range(4)]
              + ["wv%d_%d" % (t, b) for t in range(WAVES - 1) for b in range(2)]
              + ["bk%d" % t for t in range(1, WAVES + 1)])


def col(v, swapped, who):
    return Z + v * VB + who * SL + swapped * HB


def rank_program(g, core, T, topo):
    r = T.rank_of(core)
    if r is None:
        return
    cores = list(T.cores)
    sets = [[q for q in range(4) if topo.die(cores[q]) == topo.die(cores[0])],
            [q for q in range(4) if topo.die(cores[q]) != topo.die(cores[0])]]
    M = 0 if r in sets[0] else 1
    pos = sets[M].index(r)
    mate, part, pmate = sets[M][1 - pos], sets[1 - M][pos], sets[1 - M][1 - pos]
    mine = [part, r]
    theirs = [pmate, mate]

    def dst(q):
        rid, pid, _ = topo.addr(cores[q])
        return DstId(rid=rid, pnc=pid)

    def bits(es):
        return sum(1 << e for e in es)

    V, AC, PE, SY = g.vector, g.scalar, g.tensor, g.sync
    Q = {"v": [V, "sv", 0, {}], "a": [AC, "sa", 0, {}], "p": [PE, "sp", 0, {}], "g": [g, "sg", 0, {}],
         "s": [SY, None, 0, {}]}

    def wait(qn, deps):
        q = Q[qn]
        for d in deps:
            if d is not None and q[3].get(d[0], 0) < d[1]:
                q[0].wait_ge(T.sem[d[0]], d[1])
                q[3][d[0]] = d[1]

    def done(qn, inst):
        q = Q[qn]
        inst.then_inc(T.sem[q[1]], 1)
        q[2] += 1
        return (q[1], q[2])

    def ts(out, in0, s1, op0, s2=None, op1=None, deps=()):
        wait("v", deps)
        if op1 is None:
            return done("v", V.tensor_scalar(out, in0, s1, None, op0))
        return done("v", V.tensor_scalar(out, in0, s1, s2, op0, op1))

    def tt(out, a, b, op, deps=()):
        wait("v", deps)
        return done("v", V.tensor_tensor(out, a, b, op))

    def cp(out, a, deps=()):
        wait("v", deps)
        return done("v", V.tensor_copy(out, a))

    def acp(out, a, deps=()):
        wait("a", deps)
        return done("a", AC.activation(out, a, F.Copy))

    def act(out, a, scale, bias, deps=()):
        wait("a", deps)
        return done("a", AC.activation(out, a, F.Identity, bias=bias, scale=scale))

    def fill(ap, c, deps=()):
        wait("v", deps)
        return done("v", V.memset(ap, c))

    def mm(items, deps=()):
        wait("p", deps)
        inst = None
        for out, lhsT, rhs, st, sp in items:
            inst = PE.matmul(out, lhsT, rhs, st, sp)
        return done("p", inst)

    W = T.win
    sent = [0]

    def send(transfers, n, deps):
        wait("g", deps)
        g.remote_dma_fused(transfers, local_sem=T.sem.sent)
        sent[0] += n

    def half(p):
        return slice(64 * p, 64 * p + 64)

    order = [3, 0, 1, 2]
    AC.dma_start(T.pk[:, 256:257], T.kw[:]).then_inc(T.sem.lpk, 16)
    SY.dma_start(T.pk[:, 128:256], T.hm[:]).then_inc(T.sem.lpk, 16)
    AC.dma_start(T.pk[:, 0:128], T.gm[:]).then_inc(T.sem.lpk, 16)
    for n, s in enumerate(order):
        c = col(s, 0, r)
        for p in range(2):
            src = slice(s * SL + p * HB, s * SL + (p + 1) * HB)
            SY.dma_start(T.oth[half(p), s * HB:(s + 1) * HB], T.m[half(1 - M), src]).then_inc(T.sem["lo%d" % s], 16)
            AC.dma_start(W[half(p), c:c + HB], T.m[half(M), src]).then_inc(T.sem["lw%d" % s], 16)

    for s in order[1:]:
        c = col(s, 1, r)
        for p, dq in enumerate((SY, AC)):
            src = slice(s * SL + (1 - p) * HB, s * SL + (2 - p) * HB)
            dq.dma_start(W[half(p), c:c + HB], T.m[half(M), src]).then_inc(T.sem.lsw, 16)

    t_ci = done("g", g.iota(T.ci[:, 0:2], [[64, 2]], 0, 1))
    t_mf = done("g", g.iota(T.mf[:], [[1, 144]], 0, 0, allow_small_or_imprecise_dtypes=True))
    t_key = done("g", g.iota(T.key[:], [[16, 2], [32, 4], [1, 16]], 0, 0, allow_small_or_imprecise_dtypes=True))
    ID, PM, M1, M2, M3, S1, S2, S3, S4, NI, KI, K0 = [T.mats[:, i * 128:(i + 1) * 128] for i in range(12)]
    t_gh0 = fill(T.gh[:], 0.0)
    act(T.rs4[0:64, :], T.gh[0:64, 0:256], 1.0, 1.0, deps=[t_gh0])
    act(T.rst[:], T.gh[:, 0:192], 1.0, 1.0)
    k1 = act(T.uu[:], T.gh[:, 0:256], 1.0, 0.0)
    act(T.lift[:], T.gh[:, 0:CH], 1.0, LIFT)
    for i, (sh, mask) in enumerate(((4, 3), (0, 112), (6, 1), (0, 15))):
        ts(T.ci[:, 3 + i:4 + i], T.ci[:, 0:1], sh, A.logical_shift_right, mask, A.bitwise_and, deps=[t_ci])
    k = ts(T.ci[:, 2:3], T.ci[:, 1:2], 127, A.bitwise_and)
    k4 = fill(T.rs4[64:96, :], 0.0)
    k = cp(T.cf[:, 0:7], T.ci[:, 0:7], deps=[k])
    t_z = fill(W[:, 0:Z], 0.0)
    pf, px, pg, p0, ph, pq = [T.cf[:, i:i + 1] for i in (0, 2, 3, 4, 5, 6)]
    p15, flip, low, seg = [T.cf[:, i:i + 1] for i in range(8, 12)]
    k = ts(low, pg, 32.0, A.mult, deps=[k])
    ts(p15, p0, 15.0, A.add)
    t_id = ts(ID, T.mf[:, 0:128], pf, A.is_equal, deps=[t_mf])
    t_pm = ts(PM, T.mf[:, 0:128], px, A.is_equal)
    k_cf = ts(seg, ph, 16.0, A.mult, low, A.add, deps=[k])
    ts(flip, ph, 2048.0, A.mult)

    def matrices(R, pk, deps):
        for p in range(2):
            for i in range(2):
                kg = acp(T.gh[half(p), (2 * R + i) * 128 + 64 * p:(2 * R + i) * 128 + 64 * p + 64],
                         pk[half(M), i * 128 + 64 * M:i * 128 + 64 * M + 64], deps=deps)
        return kg

    def weights(jobs, deps):
        for n, pk, rows in jobs:
            for p in range(2):
                k = cp(T.wc[half(p), 8 * n:8 * n + 1], pk[half(rows), 256:257], deps=deps)
        for n, pk, rows in jobs:
            k2 = ts(T.wb[:, n * 144:(n + 1) * 144], T.mf[:], p15, A.is_equal, T.wc[:, 8 * n:8 * n + 1], A.mult, deps=[k])
        return k2

    t_w1 = weights([(2, T.pk, 1 - M), (1, T.pk, M)], [("lpk", 48), k_cf])
    ts(S1, T.key[:], seg, A.subtract, 16.0, A.is_ge, deps=[t_key])
    ts(S2, T.key[:], seg, A.is_ge)
    ts(S3, T.key[:], low, A.subtract, 32.0, A.is_ge)
    t_s = ts(S4, T.key[:], seg, A.subtract, pq, A.is_ge)
    fill(T.rs4[0:64, 0:256:4], 0.0, deps=[k1])
    fill(T.rst[:, 0:192:32], 0.0)
    fill(T.uu[:, 0:256:4], 8192.0 * STEP)
    fill(T.mats[0:32, 11 * 128:12 * 128], SL / 32 * STEP)
    fill(T.mats[32:64, 11 * 128:12 * 128], STEP / 64)
    fill(T.mats[64:96, 11 * 128:12 * 128], SL / 32)
    t_k0 = fill(T.rs4[64:96, 0:256:4], float(r), deps=[k4])
    t_g1 = matrices(1, T.pk, [("lpk", 48)])
    act(NI, ID, -1.0, 0.0, deps=[t_id])
    k = act(KI, ID, -KH, 0.0)
    others = [[mate, pmate, mine[1 - R]] for R in range(2)]
    hops = sorted(set(q - mine[R] for R in range(2) for q in others[R]))
    hop = {d: T.mats[:, (12 + n) * 128:(13 + n) * 128] for n, d in enumerate(hops)}
    for d in hops:
        act(hop[d], ID, float(d * SL), 0.0)
    items = []
    for i, terms in enumerate((((ID, S3), (NI, S2)), ((ID, S3), (NI, S1)),
                               ((ID, S1), (ID, S2), (NI, S4), (NI, S3), (KI, ID)))):
        items += [(T.px0[:, 128 * i:128 * i + 128], a, b, n == 0, n == len(terms) - 1) for n, (a, b) in enumerate(terms)]

    every = topo.engines(core, cores[part])[1::2]
    send([RemoteDMATransfer(dst_ids=[dst(part)], dma_engine_mask=bits(every), remote_sem=T.sem.apk,
                            src=T.pk[:], dst=T.pkp[:])], len(every), [("lpk", 48)])
    far = topo.engines(core, cores[part])[0::2]
    near = topo.engines(core, cores[mate])[1::2]
    for n, s in enumerate(order):
        c = col(s, 0, r)
        sem = T.sem["in%d_%d" % (s, r)]
        to = [part] if n < RELAY else [part, pmate]
        send([RemoteDMATransfer(dst_ids=[dst(q) for q in to], dma_engine_mask=bits(far), remote_sem=sem,
                                src=T.oth[:, s * HB:(s + 1) * HB], dsts=[W[:, c:c + HB] for q in to]),
              RemoteDMATransfer(dst_ids=[dst(mate)], dma_engine_mask=bits(near), remote_sem=sem,
                                src=W[:, c:c + HB], dst=W[:, c:c + HB])],
             len(far) + len(near), [("lo%d" % s, 32), ("lw%d" % s, 32)])

    def arrived(s, q):
        if q == r:
            return ("lw%d" % s, 32)
        return ("in%d_%d" % (s, q), len(topo.engines(cores[q], core)) // 2)

    freed = {}

    def swap_pe(b, v, who, deps, o=0, n=HB):
        ps = T["px%d" % b][:, 0:n]
        c, d = col(v, 0, who) + o, col(v, 1, who) + o
        kp = mm([(ps, PM, W[:, c:c + n], True, True)], deps=list(deps) + [freed.get(b), t_pm])
        freed[b] = acp(W[:, d:d + n], ps, deps=[kp])
        return freed[b]

    def swap(op, v, who, deps, o=0, n=HB):
        c, d = col(v, 0, who) + o, col(v, 1, who) + o
        op(W[half(0), d:d + n], W[half(1), c:c + n], deps=deps)
        return op(W[half(1), d:d + n], W[half(0), c:c + n])

    def swap_both(v, who, deps, x):
        c, d = col(v, 0, who), col(v, 1, who)
        ka = acp(W[half(1), d + x:d + HB], W[half(0), c + x:c + HB], deps=deps)
        cp(W[half(0), d:d + HB], W[half(1), c:c + HB], deps=deps)
        return cp(W[half(1), d:d + x], W[half(0), c:c + x]), ka

    def weigh(t, R, deps):
        n, src, c = (2, T.oth, 3 * HB) if t == R == 0 else (R, W, col(t + 3, 0, mine[R]))
        return mm([(T.pa[:, 32 * R:32 * R + 32], T.wb[:, n * 144 + 15 - q:n * 144 + 143 - q],
                    src[:, c + q:c + HB:16], q == 0, q == 15) for q in range(16)], deps=deps)

    ai, who, av, f1, jj = [T.xi[:, i * 64:(i + 1) * 64] for i in range(5)]

    def chain_front(t, ka):
        k = ts(ai, T.pa[:, 0:64], flip, A.add, deps=[ka])
        k2 = ts(av, T.pa[:, 0:64], float(((S - t) % S) * VB), A.add)
        k = ts(who, ai, 3, A.bitwise_and, deps=[k])
        ts(jj, ai, 2, A.logical_shift_right, SL - 1, A.bitwise_and)
        kh = [ts(T.hh[:, 0:64], who, float(mate), A.is_equal, deps=[k]),
              ts(T.hh[:, 64:128], who, float(pmate), A.is_equal),
              tt(T.hh[:, 128:192], who, T.pa[:, 64:128], A.is_equal) if t else
              ts(T.hh[:, 128:192], who, float(part), A.is_equal)]
        ts(f1, av, 3 * VB, A.bitwise_and, deps=[k2])
        wait("v", kh)
        kf = done("v", V.tensor_tensor_scan(T.sf[:], T.rst[:], T.hh[:], 0.0, A.mult, A.add))
        kb = done("v", V.tensor_tensor_scan(T.sb[:, ::-1], T.rst[:], T.hh[:, ::-1], 0.0, A.mult, A.add))
        return kh, kf, kb

    def open_count(deps):
        return mm([(T.pc[:, 0:256], T.mats[0:96, 11 * 128:12 * 128], T.rs4[0:96, :], True, False)], deps=deps)

    def count(t, ko, ks):
        for i in range(3):
            mm([(T.pc[:, 128 * R:128 * R + 128:4], hop[others[own][i] - mine[own]],
                 T.hh[:, 64 * i + 32 * R:64 * i + 32 * R + 32], False, False)
                for R, own in enumerate((0, 1) if t else (1, 1))]
               + [(T.pc[:, 1 + i:256:4], M3, T.hh[:, 64 * i:64 * i + 64], False, False)], deps=[ko, ks[0][i], t_m])
        for n, (mat, src) in enumerate(((M1, T.sf), (M2, T.sb))):
            kc = mm([(T.pc[:, 1 + i:256:4], mat, src[:, 64 * i:64 * i + 64], False, n == 1 and i == 2)
                     for i in range(3)], deps=[ks[n + 1]])
        return kc

    def chain_back(t, ks, kc):
        k = tt(T.uu[:, 1:256:4], f1, jj, A.add, deps=[ks[1]])
        wait("v", [k, kc])
        k = done("v", V.tensor_tensor_scan(T.us[:], T.uu[:], T.pc[:, 0:256], 0.0, A.add, A.min))
        return ts(T.off[:], T.us[:, 3:256:4], float(Z + t * VB), A.add, 0.0, A.max, deps=[k]), k

    def bank(t, kk):
        return (4 * t + kk) % 6

    def chunk(t, kk):
        if t < WAVES - 1 or kk in (2, 3):
            return kk // 2, (kk % 2) * CH, CH
        return 0, (kk % 2 + kk // 2) * CH // 2, CH // 2

    def acc(t, kk):
        return T["px%d" % bank(t, kk)][:, 0:chunk(t, kk)[2]]

    def ahead(t, kk, what, deps=()):
        R, o, n = chunk(t, kk)
        cprev, cold = col(t + 3, 0, mine[R]) + o, col(t, 0, mine[R]) + o
        wait("p", list(deps) + [freed.get(bank(t, kk))])
        if "l" in what:
            PE.matmul(acc(t, kk), ID, T.lift[:, 0:n], True, False)
        if "o" in what:
            PE.matmul(acc(t, kk), ID, W[:, cold:cold + n], False, False)
        if "g" in what:
            PE.matmul(acc(t, kk), T.gh[:, 2 * R * 128:(2 * R + 1) * 128], W[:, cprev:cprev + n], False, False)

    stores = [0]

    def store(t, src, c, rows, deps, o=0, n=HB, qn="s"):
        y = (t % S) * SL + o
        wait(qn, deps)
        for p in range(2):
            Q[qn][0].dma_start(T.y[half(rows), y + p * HB:y + p * HB + n],
                               src[half(p), c + o:c + o + n]).then_inc(T.sem.stored, 16)
            stores[0] += 16

    def hand_on(s, swapped, es, deps):
        c = col(s, swapped, part)
        send([RemoteDMATransfer(dst_ids=[dst(mate)], dma_engine_mask=bits(es), remote_sem=T.sem["in%d_%d" % (s, part)],
                                src=W[:, c:c + HB], dst=W[:, c:c + HB])], len(es), deps)

    both = topo.engines(core, cores[mate])
    weigh(0, 0, [t_w1, ("lo3", 32)])
    ka = weigh(0, 1, [arrived(3, r)])
    k = mm(items, deps=[k, t_s])
    swap(acp, 3, r, [arrived(3, r)])
    t_m = freed[0] = act(T.mats[:, 256:640], T.px0[:, 0:384], STEP, 0.0, deps=[k])
    ko = open_count([t_k0])
    swap_pe(5, 3, part, [arrived(3, part)])
    ks = chain_front(0, ka)
    kc = count(0, ko, ks)
    swap(cp, 3, mate, [arrived(3, mate)])
    k_off, k_us = chain_back(0, ks, kc)
    turned = {s: swap_pe(b, s, part, [arrived(s, part)]) for s, b in ((0, 1), (1, 4), (2, 5))}
    for s in order[:RELAY]:
        hand_on(s, 0, near, [arrived(s, part)])
    wait("g", [k_off])
    g.remote_dma_fused([RemoteDMATransfer(dst_ids=[dst(part)], dma_engine_mask=bits(far), remote_sem=T.sem.aoff,
                                          src=T.off[:, 0:32], dst=T.offp[:])], local_sem=T.sem.soff)
    k_aoff = ("soff", len(every))
    for s in TWICE:
        hand_on(s, 1, both, [turned[s]])
    t_g0 = matrices(0, T.pkp, [("apk", len(every))])
    act(T.pa[:, 64:96], T.lift[:, 0:32], 0.0, float(mine[1]), deps=[k_off])
    act(T.pa[:, 96:128], T.lift[:, 0:32], 0.0, float(mine[0]))
    act(T.rs4[64:96, 0:128:4], T.lift[64:96, 0:32], 0.0, float(part), deps=[ko])
    for p in range(2):
        k = acp(T.wc[half(p), 0:1], T.pkp[half(M), 256:257])
    for kk in (2, 3, 0, 1):
        ahead(0, kk, "log", [arrived(0, r), t_g1] + ([t_g0] if kk < 2 else []))
    for s, q in ((0, mate), (1, mate), (2, mate), (3, pmate)):
        swap(cp, s, q, [arrived(s, q)])
    k_sv, k_sa = swap_both(2, pmate, [arrived(2, pmate)], 192)
    t_w0 = ts(T.wb[:, 0:144], T.mf[:], p15, A.is_equal, T.wc[:, 0:1], A.mult, deps=[k])
    for qn in "va":
        wait(qn, [arrived(s, r) for s in order] + [("lsw", 96)]
             + [("in%d_%d" % (s, pmate), len(near) + len(both)) for s in TWICE])

    near = topo.engines(core, cores[mate])
    far = topo.engines(core, cores[part])
    n_back = len(topo.engines(cores[part], core))
    n_in = len(topo.engines(cores[mate], core))
    for t in range(WAVES):
        win = W[:, 0:Z + (t + 4) * VB]
        ready = [k_off, k_sv, k_sa, t_z]
        last = t == WAVES - 1

        def gather(op, a, b):
            if t == 0 and a < HB:
                return op(T.ref[:, a:b], win.indirect(T.offp[:, a // 16:b // 16]), deps=ready + [("aoff", len(every))])
            return op(T.ref[:, a:b], win.indirect(T.off[:, a // 16:b // 16]), deps=ready)

        def finish(kk, deps):
            R, o, n = chunk(t, kk)
            px_ = acc(t, kk)
            cs = slice(R * HB + o, R * HB + o + n)
            kh = mm([(px_, T.gh[:, (2 * R + 1) * 128:(2 * R + 2) * 128], T.ref[:, cs], False, True)], deps=deps)
            kr = act(T.rnd[:, cs], px_, 1.0, -127.5, deps=[kh])
            c = col(t + 4, 0, mine[R]) + o
            freed[bank(t, kk)] = tt(W[:, c:c + n], px_, T.rnd[:, cs], A.subtract, deps=[kr])
            return freed[bank(t, kk)]

        if 2 <= t:
            store(t - 1, W, col(t + 3, 0, r), M, [k_off])
        c0, c1 = col(t + 4, 0, mine[0]), col(t + 4, 0, mine[1])

        def back(deps, i=0, n=HB):
            o = (t % S) * HB + i * n
            send([RemoteDMATransfer(dst_ids=[dst(part)], dma_engine_mask=bits(far), remote_sem=T.sem["bk%d" % (t + i)],
                                    src=W[:, c0 + i * n:c0 + i * n + n], dst=T.back[:, o:o + n])], len(far), deps)

        def store_back(t, deps):
            store(t, T.back, (t % S) * HB, 1 - M, [("bk%d" % t, n_back)] + deps)

        if 2 <= t:
            store_back(t - 1, [])
        if last:
            ga = [gather(cp, 0, 128), gather(acp, 128, 256), gather(cp, 256, 384), gather(acp, 384, 512)]
            g2 = gather(cp, 512, 640)
            for n, kk in enumerate((0, 1, 4, 5)):
                k = finish(kk, ga[n:n + 1])
                if n % 2:
                    back([k], n // 2, CH)
            ahead(t, 2, "g")
            ahead(t, 3, "log")
            g3 = gather(acp, 640, 768)
            g4 = gather(cp, 768, 1024)
            new = [finish(2, [g2, g3]), finish(3, [g4])]
            for i in range(2):
                store(t, W, c1, M, [new[i]], i * CH, CH)
                store(t, T.back, 0, 1 - M, [("bk%d" % (t + i), n_back)], i * CH, CH, "a")
            break
        x = OPT["gv"]
        ga = [gather(cp, 0, 256), gather(acp, 256, 512)]
        gb = [gather(cp, 512, 768), gather(cp, 768, x), gather(acp, x, 1024)]
        ko = open_count([k_us, t_w0])
        ahead(t + 1, 0, "lo")
        new = [finish(0, ga[:1]), finish(1, ga[1:])]
        ahead(t + 1, 1, "lo")
        new += [finish(2, gb[:1]), finish(3, gb[1:])]
        k_own = [swap(acp, t + 4, mine[1], [new[2]], 0, CH), swap(cp, t + 4, mine[1], [new[3]], CH, CH)]
        for b, (c, deps) in enumerate(((c0, [new[1]]), (c1, [new[3]]), (col(t + 4, 1, mine[1]), k_own))):
            send([RemoteDMATransfer(dst_ids=[dst(mate)], dma_engine_mask=bits(near),
                                    remote_sem=T.sem["wv%d_%d" % (t, min(b, 1))],
                                    src=W[:, c:c + HB], dst=W[:, c:c + HB])], len(near), deps)
        if t >= 1:
            back([])
        weigh(t + 1, 0, [new[1]])
        ka = weigh(t + 1, 1, [new[3]])
        swap(acp, t + 4, mine[0], [new[1]])
        ks = chain_front(t + 1, ka)
        ahead(t + 1, 0, "g")
        ahead(t + 1, 1, "g")
        ahead(t + 1, 2, "lo")
        kc = count(t + 1, ko, ks)
        wait("v", [k_aoff])
        k_off, k_us = chain_back(t + 1, ks, kc)
        k_sa = swap(acp, t + 4, theirs[0], [("wv%d_0" % t, n_in)])
        if t + 2 == WAVES:
            ahead(t + 1, 4, "log")
            ahead(t + 1, 5, "log")
        else:
            ahead(t + 1, 2, "g")
            ahead(t + 1, 3, "log")
        k_sv = ("wv%d_1" % t, 2 * n_in)

    wait("s", [("stored", stores[0])])
    wait("g", [("sent", sent[0]), ("sv", Q["v"][2]), ("sa", Q["a"][2]), ("sp", Q["p"][2]), ("sg", Q["g"][2])])
